import numpy as np
import ml_dtypes


def mxq(x, axis, fmt="e4m3"):
    dtype, down = {"e4m3": (ml_dtypes.float8_e4m3fn, 7), "e5m2": (ml_dtypes.float8_e5m2, 14)}[fmt]
    v = np.moveaxis(np.asarray(x, np.float32).astype(ml_dtypes.bfloat16).astype(np.float64), axis, -1)
    blocks = v.reshape(v.shape[:-1] + (-1, 32))
    amax = np.abs(blocks).max(-1, keepdims=True)
    byte = np.maximum(np.where(amax > 0, np.frexp(amax)[1] - 1 + 127, 0) - down, 1)
    scale = np.exp2(byte - 127.0)
    codes = (blocks / scale).astype(np.float32).astype(dtype).astype(np.float64)
    return np.moveaxis((codes * scale).reshape(v.shape), -1, axis)


WIDE = False


def mx_kscale(k):
    if not WIDE:
        return np.ones(k)
    levels = np.array([10, -10, 5, -5, 0])
    if k % 512:
        return np.exp2(np.random.permutation(np.resize(levels, k // 32))).repeat(32)
    a = np.empty((k // 512, 16))
    for p in range(k // 512):
        a[p, :8] = np.random.permutation(np.resize(levels, 8))
        for g in range(8):
            far = levels[np.abs(levels - a[p, g]) >= 10]
            a[p, g + 8] = far[np.random.randint(len(far))]
    return np.exp2(a.ravel()).repeat(32)


BF16 = ml_dtypes.bfloat16


def bf(x):
    return np.asarray(x, np.float32).astype(BF16)


def f64(x):
    return np.asarray(x).astype(np.float64)


U, V, KU, KV, L = 512, 2048, 1024, 512, 1024

LV_CAP = 2.0


def setup_inputs():
    s, r, t = mx_kscale(KU), mx_kscale(KV), mx_kscale(L)
    return {"xu": bf(np.random.standard_normal((U, KU)) * s),
            "wu_mean": bf(np.random.standard_normal((KU, L)) / np.sqrt(KU) / s[:, None]),
            "wu_lv": bf(np.random.standard_normal((KU, L)) / np.sqrt(KU) / s[:, None]),
            "bu_mean": bf(0.3 * np.random.standard_normal(L)),
            "bu_lv": bf(0.3 * np.random.standard_normal(L)),
            "noise_u": bf(np.random.standard_normal((U, L))),
            "gain_u": bf((1 + 0.1 * np.random.standard_normal(L)) * t),
            "xv": bf(np.random.standard_normal((V, KV)) * r),
            "wv_mean": bf(np.random.standard_normal((KV, L)) / np.sqrt(KV) / r[:, None]),
            "wv_lv": bf(np.random.standard_normal((KV, L)) / np.sqrt(KV) / r[:, None]),
            "bv_mean": bf(0.3 * np.random.standard_normal(L)),
            "bv_lv": bf(0.3 * np.random.standard_normal(L)),
            "noise_v": bf(np.random.standard_normal((V, L))),
            "gain_v": bf((1 + 0.1 * np.random.standard_normal(L)) / t),
            "cu": bf(0.5 * np.random.standard_normal(U)),
            "cv": bf(0.5 * np.random.standard_normal(V))}


def soft_cap(a):
    return LV_CAP * np.tanh(a / LV_CAP)


def kl_rows(mean, lv):
    return 0.5 * np.mean(mean * mean + np.exp(lv) - 1.0 - lv, axis=1)


def reference(xu, wu_mean, wu_lv, bu_mean, bu_lv, noise_u, gain_u,
              xv, wv_mean, wv_lv, bv_mean, bv_lv, noise_v, gain_v, cu, cv):
    xuq = mxq(f64(xu), 1, "e4m3")
    mean_u = (xuq @ mxq(f64(wu_mean), 0, "e4m3")) + f64(bu_mean)
    lv_u = soft_cap((xuq @ mxq(f64(wu_lv), 0, "e4m3")) + f64(bu_lv))
    zu = (mean_u + np.exp(0.5 * lv_u) * f64(noise_u)) * f64(gain_u)
    xvq = mxq(f64(xv), 1, "e4m3")
    mean_v = (xvq @ mxq(f64(wv_mean), 0, "e4m3")) + f64(bv_mean)
    lv_v = soft_cap((xvq @ mxq(f64(wv_lv), 0, "e4m3")) + f64(bv_lv))
    zv = (mean_v + np.exp(0.5 * lv_v) * f64(noise_v)) * f64(gain_v)
    score = (mxq(zu, 1, "e4m3") @ mxq(zv, 1, "e4m3").T) / np.sqrt(L)
    logit = score + f64(cu)[:, None] + f64(cv)[None, :]
    prob = 1.0 / (1.0 + np.exp(-logit))
    return prob, kl_rows(mean_u, lv_u), kl_rows(mean_v, lv_v)

@@ -1,0 +1,490 @@
+import math
+from contextlib import ExitStack
+
+import concourse.mybir as mybir
+from concourse.masks import make_identity
+
+U, V, KU, KV, L = 512, 2048, 1024, 512, 1024
+FLOPS = 2 * (2 * U * KU * L + 2 * V * KV * L + U * V * L)
+
+F32 = mybir.dt.float32
+BF16 = mybir.dt.bfloat16
+U32 = mybir.dt.uint32
+U8 = mybir.dt.uint8
+FP8X4 = mybir.dt.float8_e4m3fn_x4
+ALU = mybir.AluOpType
+ACTF = mybir.ActivationFunctionType
+AX = mybir.AxisListType
+
+P = 128
+ROWS = 512
+HALF = 512
+N_BLOCKS = 5
+N_STEPS = 4 * N_BLOCKS
+R2 = math.sqrt(0.5)
+BLOCKS = ("v", "v", "u", "v", "v")
+V_INDEX = (0, 1, 0, 2, 3)
+KL_COL = (4, 8, 0, 12, 16)
+
+
+def tile_variational_link_decoder_f5_kernel(
+    tc, xu, wu_mean, wu_lv, bu_mean, bu_lv, noise_u, gain_u,
+    xv, wv_mean, wv_lv, bv_mean, bv_lv, noise_v, gain_v, cu, cv,
+    prob, kl_u, kl_v,
+):
+    nc = tc.nc
+    with ExitStack() as ctx:
+        sb = ctx.enter_context(tc.tile_pool(name="sb", bufs=1))
+        ps = ctx.enter_context(tc.psum_pool(name="ps", bufs=1))
+        ctx.enter_context(tc.manual_schedule())
+
+        def sbt(shape, dt, tag, bufs=1):
+            return sb.tile(shape, dt, name=tag, tag=tag, bufs=bufs, align_bytes=64)
+
+        def bank(tag, bufs=1):
+            return ps.tile([P, 512], F32, name=tag, tag=tag, bufs=bufs)
+
+        zero1 = sbt([P, 1], F32, "zero1")
+        nc.vector.memset(zero1[:], 0.0)
+        vecs = sbt([P, L], BF16, "vecs")
+        nc.vector.memset(vecs[:], 0.0)
+        cur = sbt([P, P], BF16, "cur")
+        nc.vector.memset(cur[:], 0.0)
+        dummy = sbt([P, 1], F32, "dummy")
+        nc.scalar.activation(dummy[:], zero1[:], ACTF.Exp)
+
+        x_raw = {}
+        w_raw = {}
+        n_raw = {}
+
+        def load_x(key, source, row0, col0):
+            raw = sbt([P, 4, 512], BF16, "x_raw", 3)
+            for half in range(2):
+                r0 = row0 + 256 * half
+                nc.sync.dma_start(
+                    out=raw[:, 2 * half : 2 * half + 2, :],
+                    in_=source[r0 : r0 + 256, col0 : col0 + 512].rearrange("(s p) k -> p s k", p=P),
+                )
+            x_raw[key] = raw
+
+        def load_w(key, source, c, g):
+            raw = sbt([P, 4, 512], BF16, "w_raw", 5)
+            nc.sync.dma_start(
+                out=raw[:],
+                in_=source[512 * c : 512 * c + 512, 512 * g : 512 * g + 512].rearrange("(p j) c -> p j c", j=4),
+            )
+            w_raw[key] = raw
+
+        def load_noise(h):
+            b, g = divmod(h, 2)
+            source = noise_u if BLOCKS[b] == "u" else noise_v
+            r0 = ROWS * V_INDEX[b]
+            raw = sbt([P, 4, 512], BF16, "n_raw", 4)
+            nc.sync.dma_start(
+                out=raw[:],
+                in_=source[r0 : r0 + ROWS, 512 * g : 512 * g + 512].rearrange("(s p) c -> p s c", p=P),
+            )
+            n_raw[h] = raw
+
+        load_x(0, xv, 0, 0)
+        load_w(("v", 0, 0, 0), wv_lv, 0, 0)
+        load_w(("v", 1, 0, 0), wv_mean, 0, 0)
+        load_noise(0)
+        load_w(("v", 0, 0, 1), wv_lv, 0, 1)
+        load_w(("v", 1, 0, 1), wv_mean, 0, 1)
+        load_x(1, xv, 512, 0)
+        load_noise(1)
+        u_chunks = [("u", m, c, g) for g in range(2) for m in range(2) for c in range(2)]
+        u_src = (wu_lv, wu_mean)
+
+        def load_u_chunk(i):
+            key = u_chunks[i]
+            load_w(key, u_src[key[1]], key[2], key[3])
+
+        load_u_chunk(0)
+        load_x((2, 0), xu, 0, 0)
+        load_noise(2)
+        load_noise(3)
+
+        for r, vec in enumerate((bu_mean, bu_lv, gain_u, bv_mean, bv_lv, gain_v)):
+            nc.scalar.dma_start(out=vecs[r : r + 1, :], in_=vec.rearrange("(o l) -> o l", o=1))
+        nc.scalar.dma_start(out=cur[0:4, :], in_=cu.rearrange("(i p) -> i p", p=P))
+        cvb = sbt([P, V], BF16, "cvb")
+
+        ident = sbt([P, P], F32, "ident")
+        make_identity(nc, ident[:])
+
+        wq = {
+            "v": (sbt([P, 2, 1, L], U32, "wv_codes"), sbt([P, 2, 1, L], U8, "wv_scales")),
+            "u": (sbt([P, 2, 2, L], U32, "wu_codes"), sbt([P, 2, 2, L], U8, "wu_scales")),
+        }
+        xq = {}
+        zq = [
+            (sbt([P, 2, 512], U32, "z_codes%d" % b), sbt([P, 2, 512], U8, "z_scales%d" % b))
+            for b in range(N_BLOCKS)
+        ]
+        grp = {}
+
+        def group_w(key, engine):
+            raw = w_raw.pop(key)
+            t = sbt([P, 2048], BF16, "grp", 4)
+            dst = t[:].rearrange("p (t m j) -> p t m j", t=4, j=4)
+            src = raw[:].rearrange("p j (m t) -> p t m j", t=4)
+            if engine == "v":
+                nc.vector.tensor_copy(out=dst, in_=src)
+            else:
+                nc.gpsimd.tensor_scalar(dst, src, 1.0, 0.0, ALU.mult, ALU.add)
+            grp[key] = t
+
+        def quant_w(key):
+            kind, m, c, g = key
+            codes, scales = wq[kind]
+            nc.vector.quantize_mx(
+                out=codes[:, m, c, 512 * g : 512 * g + 512].bitcast(FP8X4),
+                scales=scales[:, m, c, 512 * g : 512 * g + 512],
+                in_=grp.pop(key)[:],
+            )
+
+        x_bank = {}
+
+        def turn_x(key, half, tag="xt"):
+            words = x_raw[key][:].bitcast(F32)
+            bk = bank(tag)
+            for s in range(2):
+                for w in range(2):
+                    o = 256 * s + 128 * w
+                    nc.tensor.transpose(bk[:, o : o + 128], words[:, 2 * half + s, w:256:2], ident[:])
+            x_bank[key, half] = bk
+
+        def copy_x(key, half, engine):
+            if half == 0:
+                grp[key] = sbt([P, 2048], BF16, "grp", 4)
+            dst = grp[key][:].bitcast(F32)[:, 512 * half : 512 * half + 512].rearrange(
+                "p (s r w) -> p s r w", s=2, w=2)
+            src = x_bank.pop((key, half))[:].rearrange("p (s w r) -> p s r w", s=2, w=2)
+            if engine == "v":
+                nc.vector.tensor_copy(out=dst, in_=src)
+            else:
+                nc.scalar.copy(out=dst, in_=src)
+
+        def quant_x(key):
+            codes = sbt([P, 512], U32, "x_codes", 4)
+            scales = sbt([P, 512], U8, "x_scales", 4)
+            nc.vector.quantize_mx(out=codes[:].bitcast(FP8X4), scales=scales[:], in_=grp.pop(key)[:])
+            xq[key] = (codes, scales)
+
+        def stage1(bk, b, m, g, t):
+            kind = BLOCKS[b]
+            codes, scales = wq[kind]
+            n = 2 if kind == "u" else 1
+            lo = 512 * g + 128 * t
+            for c in range(n):
+                xc, xs = xq[(b, c) if kind == "u" else b]
+                nc.tensor.matmul_mx(
+                    out=bk[:],
+                    lhsT=codes[:, m, c, lo : lo + 128].bitcast(FP8X4),
+                    lhsT_scale=scales[:, m, c, lo : lo + 128],
+                    rhs=xc[:].bitcast(FP8X4),
+                    rhs_scale=xs[:],
+                    start=(c == 0),
+                    stop=(c == n - 1),
+                )
+
+        lv_bank, mean_bank, noise_bank = {}, {}, {}
+
+        def emit_lv(p):
+            h, u = divmod(p, 2)
+            for k in range(2):
+                bk = bank("lv", 2)
+                stage1(bk, h // 2, 0, h % 2, 2 * u + k)
+                lv_bank[p, k] = bk
+
+        def emit_mean(p):
+            h, u = divmod(p, 2)
+            for k in range(2):
+                bk = bank("mean", 2)
+                stage1(bk, h // 2, 1, h % 2, 2 * u + k)
+                mean_bank[p, k] = bk
+
+        def emit_noise(p):
+            h, u = divmod(p, 2)
+            words = n_raw[h][:].bitcast(F32)
+            bk = bank("nt")
+            for s in range(4):
+                nc.tensor.transpose(bk[:, 128 * s : 128 * s + 128], words[:, s, u:256:2], ident[:])
+            noise_bank[p] = bk
+
+        turn_x(0, 0, "xt")
+        turn_x(0, 1, "nt")
+        pb = bank("kl")
+        vw = vecs[:].bitcast(F32)
+        for a in range(4):
+            lo = 256 * (a // 2)
+            nc.tensor.transpose(pb[:, 128 * a : 128 * a + 128], vw[:, lo + a % 2 : lo + 256 : 2], ident[:])
+        curf = sbt([P, P], F32, "curf")
+        cb = bank("dec")
+
+        copy_x(0, 0, "s")
+        copy_x(0, 1, "s")
+        group_w(("v", 0, 0, 0), "v")
+        nc.vector.tensor_copy(out=curf[:], in_=cur[:])
+        nc.tensor.transpose(cb[:, 0:128], curf[:], ident[:])
+        quant_w(("v", 0, 0, 0))
+        quant_x(0)
+        par = sbt([P, 6, 8], F32, "par")
+        nc.vector.tensor_copy(
+            out=par[:].rearrange("p r (a e) -> p r a e", e=2),
+            in_=pb[:].bitcast(BF16).rearrange("p (a r e) -> p r a e", a=4, e=2)[:, 0:6],
+        )
+        group_w(("v", 1, 0, 0), "v")
+        nhb = sbt([P, 2, 8], F32, "nhb")
+        rb = sbt([P, 2, 8], F32, "rb")
+        for i in range(2):
+            nc.vector.tensor_scalar(nhb[:, i, :], par[:, 3 * i + 1, :], -0.5, None, ALU.mult)
+            nc.vector.tensor_scalar(rb[:, i, :], par[:, 3 * i, :], R2, None, ALU.mult)
+        nln2 = sbt([P, 1], F32, "nln2")
+        nc.vector.tensor_scalar(nln2[:], zero1[:], -math.log(2.0), None, ALU.add)
+        quant_w(("v", 1, 0, 0))
+        hcu = sbt([P, 4], F32, "hcu")
+        nc.vector.tensor_scalar(hcu[:], cb[:, 0:4], 0.5, None, ALU.mult)
+        load_u_chunk(1)
+        load_u_chunk(2)
+        load_x((2, 1), xu, 0, 512)
+
+        emit_lv(0)
+        emit_noise(0)
+        emit_mean(0)
+
+        nth, hm2, he2, zz, zbf = {}, {}, {}, {}, {}
+        red = sbt([P, 2, 20], F32, "red")
+        kl_bank = {}
+
+        def emit_kl(h, s):
+            if s == 0:
+                kl_bank[h] = bank("kl")
+            n = 0
+            for part in (nth[h], hm2[h], he2[h]):
+                for t in range(4):
+                    nc.tensor.matmul(
+                        out=kl_bank[h][:, 128 * s : 128 * s + 128],
+                        lhsT=part[:, t, 128 * s : 128 * s + 128],
+                        rhs=ident[:],
+                        start=(n == 0),
+                        stop=(n == 11),
+                        is_transpose=True,
+                    )
+                    n += 1
+
+        def reduce_kl(h):
+            b, g = divmod(h, 2)
+            j = KL_COL[b]
+            nc.vector.tensor_reduce(
+                out=red[:, g, j : j + 4],
+                in_=kl_bank.pop(h)[:].rearrange("p (s c) -> p s c", s=4),
+                axis=AX.X,
+                op=ALU.add,
+            )
+
+        def gain_of(h):
+            b, g = divmod(h, 2)
+            row = 2 if BLOCKS[b] == "u" else 5
+            return par[:, row, 4 * g : 4 * g + 4].unsqueeze(1)
+
+        def quant_z(h, w0=0, w1=512):
+            b, g = divmod(h, 2)
+            codes, scales = zq[b]
+            nc.vector.quantize_mx(
+                out=codes[:, g, w0:w1].bitcast(FP8X4),
+                scales=scales[:, g, w0:w1],
+                in_=zbf[h][:, 4 * w0 : 4 * w1],
+            )
+
+        dec_bank = {}
+
+        def emit_dec(b, i, tag, bufs=1):
+            bk = bank(tag, bufs)
+            for g in range(2):
+                nc.tensor.matmul_mx(
+                    out=bk[:],
+                    lhsT=zq[2][0][:, g, 128 * i : 128 * i + 128].bitcast(FP8X4),
+                    lhsT_scale=zq[2][1][:, g, 128 * i : 128 * i + 128],
+                    rhs=zq[b][0][:, g, :].bitcast(FP8X4),
+                    rhs_scale=zq[b][1][:, g, :],
+                    start=(g == 0),
+                    stop=(g == 1),
+                )
+            dec_bank[b, i] = bk
+
+        logit = {}
+
+        def dec_add(b, i):
+            t = sbt([P, 512], F32, "logit", 5)
+            v0 = 512 * V_INDEX[b]
+            nc.vector.scalar_tensor_tensor(
+                t[:], dec_bank.pop((b, i))[:], 1.0 / math.sqrt(L), cvb[:, v0 : v0 + 512], ALU.mult, ALU.add)
+            logit[b, i] = t
+
+        def dec_tanh(b, i):
+            t = logit[b, i]
+            nc.scalar.activation(t[:], t[:], ACTF.Tanh, bias=hcu[:, i : i + 1], scale=0.5)
+
+        def dec_store(b, i):
+            t = logit.pop((b, i))
+            v0 = 512 * V_INDEX[b]
+            nc.gpsimd.tensor_scalar(t[:], t[:], 0.5, 0.5, ALU.mult, ALU.add)
+            nc.sync.dma_start(out=prob[128 * i : 128 * i + 128, v0 : v0 + 512], in_=t[:])
+
+        pre = {p: [] for p in range(N_STEPS)}
+        pool_work = {p: [] for p in range(N_STEPS)}
+        x_work = {p: [] for p in range(N_STEPS)}
+        loads = {p: [] for p in range(N_STEPS)}
+        dec_work = {p: [] for p in range(N_STEPS)}
+
+        def later(table, p, func, *args):
+            table[p].append((func, args))
+
+        def run(table, p):
+            for func, args in table[p]:
+                func(*args)
+
+        for m in range(2):
+            later(pre, m, group_w, ("v", m, 0, 1), "v")
+        for key, p in ((1, 0), ((2, 0), 2), ((2, 1), 4), (3, 7), (4, 10)):
+            later(x_work, p, turn_x, key, 0)
+            later(x_work, p + 1, turn_x, key, 1)
+            later(pre, p + 1, copy_x, key, 0, "v")
+            later(pre, p + 2, copy_x, key, 1, "v")
+        for i in range(8):
+            if i % 2:
+                later(pre, i + 1, group_w, u_chunks[i], "v")
+            else:
+                later(pool_work, i + 1, group_w, u_chunks[i], "p")
+        for m in range(2):
+            later(pre, m, quant_w, ("v", m, 0, 1))
+        for h in range(2 * N_BLOCKS - 1):
+            later(pre, 2 * h + 3, quant_z, h)
+        for i in range(8):
+            later(pre, i + 2, quant_w, u_chunks[i])
+        for key, p in ((1, 0), ((2, 0), 2), ((2, 1), 4), (3, 7), (4, 10)):
+            later(pre, p + 2, quant_x, key)
+        later(loads, 0, load_noise, 4)
+        later(loads, 0, load_u_chunk, 3)
+        later(loads, 1, load_u_chunk, 4)
+        later(loads, 1, load_u_chunk, 5)
+        later(loads, 2, load_u_chunk, 6)
+        later(loads, 2, load_noise, 5)
+        later(loads, 3, load_u_chunk, 7)
+        later(loads, 3, load_x, 3, xv, 1024, 0)
+        later(loads, 4, load_noise, 6)
+        later(loads, 5, load_x, 4, xv, 1536, 0)
+        later(loads, 6, load_noise, 7)
+        later(loads, 8, load_noise, 8)
+        later(loads, 10, load_noise, 9)
+
+        dec_list = {}
+        for n, (b, i) in enumerate([(b, i) for b in (0, 1, 3) for i in range(4)]):
+            p = 13 + n // 2
+            dec_list.setdefault(p, []).append((b, i))
+            later(dec_work, p, emit_dec, b, i, "xt" if n % 2 else "dec")
+            later(pre, p + 1, dec_add, b, i)
+
+        for p in range(N_STEPS):
+            h, u = divmod(p, 2)
+            b, g = divmod(h, 2)
+            kind = 0 if BLOCKS[b] == "u" else 1
+            if u == 0:
+                nth[h] = sbt([P, 4, 512], F32, "nth", 2)
+                hm2[h] = sbt([P, 4, 512], F32, "hm2", 2)
+                he2[h] = sbt([P, 4, 512], F32, "he2", 2)
+                zz[h] = sbt([P, 4, 512], F32, "zz", 2)
+            for k in range(2):
+                t = 2 * u + k
+                c = 4 * g + t
+                nc.scalar.activation(
+                    nth[h][:, t, :], lv_bank.pop((p, k))[:], ACTF.Tanh,
+                    bias=nhb[:, kind, c : c + 1], scale=-0.5)
+            pair = nth[h][:, 2 * u : 2 * u + 2, :].rearrange("p k w -> p (k w)")
+            e = sbt([P, 2, 512], F32, "e", 2)
+            nc.scalar.activation(e[:].rearrange("p k w -> p (k w)"), pair, ACTF.Exp, scale=-1.0)
+
+            run(pool_work, p)
+            run(pre, p)
+            if p + 1 < N_STEPS:
+                emit_lv(p + 1)
+            if h >= 1:
+                emit_kl(h - 1, 2 * u)
+                emit_kl(h - 1, 2 * u + 1)
+            run(x_work, p)
+
+            for k in range(2):
+                t = 2 * u + k
+                c = 4 * g + t
+                nc.scalar.activation(
+                    hm2[h][:, t, :], mean_bank[p, k][:], ACTF.Square,
+                    bias=rb[:, kind, c : c + 1], scale=R2)
+            for b2, i2 in dec_list.get(p - 1, []):
+                dec_tanh(b2, i2)
+                dec_store(b2, i2)
+            nc.scalar.activation(
+                he2[h][:, 2 * u : 2 * u + 2, :].rearrange("p k w -> p (k w)"), pair, ACTF.Exp,
+                bias=nln2[:], scale=-2.0)
+
+            nview = noise_bank.pop(p)[:].bitcast(BF16).rearrange("p (r e) -> p r e", e=2)
+            for k in range(2):
+                nc.vector.tensor_tensor(e[:, k, :], e[:, k, :], nview[:, :, k], ALU.mult)
+            for k in range(2):
+                t = 2 * u + k
+                c = 4 * g + t
+                nc.vector.scalar_tensor_tensor(
+                    zz[h][:, t, :], mean_bank.pop((p, k))[:], par[:, 3 * kind, c : c + 1], e[:, k, :],
+                    ALU.add, ALU.add)
+            if u == 1 and h >= 1:
+                reduce_kl(h - 1)
+            if p + 1 < N_STEPS:
+                emit_noise(p + 1)
+                emit_mean(p + 1)
+            run(dec_work, p)
+            run(loads, p)
+            if p == 4:
+                nc.sync.dma_start(out=cvb[:], in_=cv.partition_broadcast(P))
+            if u == 1:
+                zbf[h] = sbt([P, 2048], BF16, "zbf", 2)
+                if p + 1 < N_STEPS:
+                    nc.gpsimd.tensor_tensor(
+                        zbf[h][:].rearrange("p (w t) -> p w t", t=4),
+                        zz[h][:].rearrange("p t w -> p w t"),
+                        gain_of(h).to_broadcast([P, 512, 4]),
+                        ALU.mult)
+
+        last = 2 * N_BLOCKS - 1
+        for half in range(2):
+            w0 = 256 * half
+            nc.vector.tensor_tensor(
+                zbf[last][:, 4 * w0 : 4 * w0 + 1024].rearrange("p (w t) -> p w t", t=4),
+                zz[last][:, :, w0 : w0 + 256].rearrange("p t w -> p w t"),
+                gain_of(last).to_broadcast([P, 256, 4]),
+                ALU.mult)
+        quant_z(last, 0, 256)
+        quant_z(last, 256, 512)
+        for s in range(3):
+            emit_kl(last, s)
+        tail_tags = (("dec", 1), ("xt", 1), ("lv", 2), ("lv", 2))
+        for i in range(4):
+            emit_dec(4, i, tail_tags[i][0], tail_tags[i][1])
+        emit_kl(last, 3)
+        for i in range(4):
+            dec_add(4, i)
+            dec_tanh(4, i)
+            dec_store(4, i)
+        reduce_kl(last)
+        klc = sbt([P, P], F32, "klc")
+        nc.vector.memset(klc[:], 0.0)
+        kls = sbt([P, 20], F32, "kls")
+        nc.vector.tensor_tensor(kls[:], red[:, 0, :], red[:, 1, :], ALU.add)
+        nc.vector.tensor_scalar(klc[:, 0:20], kls[:], 1.0 / L, -0.5, ALU.mult, ALU.add)
+        kb = bank("nt")
+        nc.tensor.transpose(kb[:, 0:128], klc[:], ident[:])
+        klt = sbt([P, P], F32, "klt")
+        nc.vector.tensor_copy(out=klt[:], in_=kb[:, 0:128])
+        nc.sync.dma_start(out=kl_u.rearrange("(j r) -> j r", r=P), in_=klt[0:4, :])
+        nc.sync.dma_start(out=kl_v.rearrange("(j r) -> j r", r=P), in_=klt[4:20, :])

@@ -18,13 +18,12 @@ AX = mybir.AxisListType
 
 P = 128
 ROWS = 512
-HALF = 512
 N_BLOCKS = 5
-N_STEPS = 4 * N_BLOCKS
-R2 = math.sqrt(0.5)
-BLOCKS = ("v", "v", "u", "v", "v")
-V_INDEX = (0, 1, 0, 2, 3)
-KL_COL = (4, 8, 0, 12, 16)
+N_TILES = 4 * N_BLOCKS
+BLOCKS = ("v", "v", "v", "u", "v")
+V_INDEX = (0, 1, 2, 0, 3)
+KL_COL = (4, 8, 12, 0, 16)
+U_BLOCK = 3
 
 
 def tile_variational_link_decoder_f5_kernel(
@@ -41,8 +40,10 @@ def tile_variational_link_decoder_f5_kernel(
         def sbt(shape, dt, tag, bufs=1):
             return sb.tile(shape, dt, name=tag, tag=tag, bufs=bufs, align_bytes=64)
 
-        def bank(tag, bufs=1):
-            return ps.tile([P, 512], F32, name=tag, tag=tag, bufs=bufs)
+        BANKS = {"lv": 2, "mean": 2, "z": 2, "xt": 1, "dec": 1}
+
+        def bank(tag):
+            return ps.tile([P, 512], F32, name=tag, tag=tag, bufs=BANKS[tag])
 
         zero1 = sbt([P, 1], F32, "zero1")
         nc.vector.memset(zero1[:], 0.0)
@@ -52,10 +53,15 @@ def tile_variational_link_decoder_f5_kernel(
         nc.vector.memset(cur[:], 0.0)
         dummy = sbt([P, 1], F32, "dummy")
         nc.scalar.activation(dummy[:], zero1[:], ACTF.Exp)
+        sel = sbt([P, 4, P], BF16, "sel")
+        nc.vector.memset(sel[:], 0.0)
+        for q in range(4):
+            nc.vector.memset(sel[32 * q : 32 * q + 1, q, :], 1.0)
+        sums = [sbt([P, 2, N_TILES], F32, "sum_%s" % name) for name in ("th", "sq")]
+        for t in sums:
+            nc.vector.memset(t[:], 0.0)
 
-        x_raw = {}
-        w_raw = {}
-        n_raw = {}
+        x_raw, w_raw, n_raw = {}, {}, {}
 
         def load_x(key, source, row0, col0):
             raw = sbt([P, 4, 512], BF16, "x_raw", 3)
@@ -75,38 +81,37 @@ def tile_variational_link_decoder_f5_kernel(
             )
             w_raw[key] = raw
 
-        def load_noise(h):
-            b, g = divmod(h, 2)
+        def load_noise(i):
+            b, s = divmod(i, 4)
             source = noise_u if BLOCKS[b] == "u" else noise_v
-            r0 = ROWS * V_INDEX[b]
-            raw = sbt([P, 4, 512], BF16, "n_raw", 4)
-            nc.sync.dma_start(
-                out=raw[:],
-                in_=source[r0 : r0 + ROWS, 512 * g : 512 * g + 512].rearrange("(s p) c -> p s c", p=P),
-            )
-            n_raw[h] = raw
+            r0 = ROWS * V_INDEX[b] + P * s
+            raw = sbt([P, L], BF16, "n_raw", 6)
+            nc.sync.dma_start(out=raw[:], in_=source[r0 : r0 + P, :])
+            n_raw[i] = raw
 
-        load_x(0, xv, 0, 0)
-        load_w(("v", 0, 0, 0), wv_lv, 0, 0)
-        load_w(("v", 1, 0, 0), wv_mean, 0, 0)
-        load_noise(0)
-        load_w(("v", 0, 0, 1), wv_lv, 0, 1)
-        load_w(("v", 1, 0, 1), wv_mean, 0, 1)
-        load_x(1, xv, 512, 0)
-        load_noise(1)
-        u_chunks = [("u", m, c, g) for g in range(2) for m in range(2) for c in range(2)]
+        u_chunks = [("u", m, c, g) for m in range(2) for g in range(2) for c in range(2)]
         u_src = (wu_lv, wu_mean)
 
         def load_u_chunk(i):
             key = u_chunks[i]
             load_w(key, u_src[key[1]], key[2], key[3])
 
+        load_x(0, xv, 0, 0)
+        load_w(("v", 0, 0, 0), wv_lv, 0, 0)
+        load_w(("v", 0, 0, 1), wv_lv, 0, 1)
+        load_w(("v", 1, 0, 0), wv_mean, 0, 0)
+        load_noise(0)
+        load_w(("v", 1, 0, 1), wv_mean, 0, 1)
+        load_noise(1)
+        load_x(1, xv, 512, 0)
         load_u_chunk(0)
-        load_x((2, 0), xu, 0, 0)
         load_noise(2)
         load_noise(3)
+        load_x(2, xv, 1024, 0)
+        load_noise(4)
+        load_noise(5)
 
-        for r, vec in enumerate((bu_mean, bu_lv, gain_u, bv_mean, bv_lv, gain_v)):
+        for r, vec in ((0, bv_lv), (32, bv_mean), (1, gain_v), (64, bu_lv), (96, bu_mean), (2, gain_u)):
             nc.scalar.dma_start(out=vecs[r : r + 1, :], in_=vec.rearrange("(o l) -> o l", o=1))
         nc.scalar.dma_start(out=cur[0:4, :], in_=cu.rearrange("(i p) -> i p", p=P))
         cvb = sbt([P, V], BF16, "cvb")
@@ -132,8 +137,11 @@ def tile_variational_link_decoder_f5_kernel(
             src = raw[:].rearrange("p j (m t) -> p t m j", t=4)
             if engine == "v":
                 nc.vector.tensor_copy(out=dst, in_=src)
+            elif engine == "s":
+                nc.scalar.copy(out=dst, in_=src)
             else:
-                nc.gpsimd.tensor_scalar(dst, src, 1.0, 0.0, ALU.mult, ALU.add)
+                for t4 in range(4):
+                    nc.gpsimd.tensor_scalar(dst[:, t4], src[:, t4], 1.0, 0.0, ALU.mult, ALU.add)
             grp[key] = t
 
         def quant_w(key):
@@ -173,141 +181,179 @@ def tile_variational_link_decoder_f5_kernel(
             nc.vector.quantize_mx(out=codes[:].bitcast(FP8X4), scales=scales[:], in_=grp.pop(key)[:])
             xq[key] = (codes, scales)
 
-        def stage1(bk, b, m, g, t):
+        def stage1(bk, i, m, g):
+            b, s = divmod(i, 4)
             kind = BLOCKS[b]
             codes, scales = wq[kind]
             n = 2 if kind == "u" else 1
-            lo = 512 * g + 128 * t
             for c in range(n):
                 xc, xs = xq[(b, c) if kind == "u" else b]
                 nc.tensor.matmul_mx(
                     out=bk[:],
-                    lhsT=codes[:, m, c, lo : lo + 128].bitcast(FP8X4),
-                    lhsT_scale=scales[:, m, c, lo : lo + 128],
-                    rhs=xc[:].bitcast(FP8X4),
-                    rhs_scale=xs[:],
+                    lhsT=xc[:, P * s : P * s + P].bitcast(FP8X4),
+                    lhsT_scale=xs[:, P * s : P * s + P],
+                    rhs=codes[:, m, c, 512 * g : 512 * g + 512].bitcast(FP8X4),
+                    rhs_scale=scales[:, m, c, 512 * g : 512 * g + 512],
                     start=(c == 0),
                     stop=(c == n - 1),
                 )
 
-        lv_bank, mean_bank, noise_bank = {}, {}, {}
+        lv_bank, mean_bank, z_bank = {}, {}, {}
+        th, e_of, en_of, m_of, em_of, zbf = {}, {}, {}, {}, {}, {}
+        junk = sbt([P, 2 * L], F32, "junk")
+        bias = {}
 
-        def emit_lv(p):
-            h, u = divmod(p, 2)
-            for k in range(2):
-                bk = bank("lv", 2)
-                stage1(bk, h // 2, 0, h % 2, 2 * u + k)
-                lv_bank[p, k] = bk
+        def kind_of(i):
+            return BLOCKS[i // 4]
 
-        def emit_mean(p):
-            h, u = divmod(p, 2)
-            for k in range(2):
-                bk = bank("mean", 2)
-                stage1(bk, h // 2, 1, h % 2, 2 * u + k)
-                mean_bank[p, k] = bk
+        def emit_lv(i, g):
+            bk = bank("lv")
+            stage1(bk, i, 0, g)
+            lv_bank[i, g] = bk
 
-        def emit_noise(p):
-            h, u = divmod(p, 2)
-            words = n_raw[h][:].bitcast(F32)
-            bk = bank("nt")
-            for s in range(4):
-                nc.tensor.transpose(bk[:, 128 * s : 128 * s + 128], words[:, s, u:256:2], ident[:])
-            noise_bank[p] = bk
+        def emit_mean(i, g):
+            bk = bank("mean")
+            stage1(bk, i, 1, g)
+            mean_bank[i, g] = bk
+
+        def lv_add(i, g):
+            if g == 0:
+                th[i] = sbt([P, L], F32, "th", 2)
+            nc.vector.tensor_tensor(
+                th[i][:, 512 * g : 512 * g + 512], lv_bank.pop((i, g))[:],
+                bias[kind_of(i), 0][:, 512 * g : 512 * g + 512], ALU.add)
+
+        def new_em(i):
+            em = sbt([P, 2, L], F32, "em", 4)
+            e_of[i], m_of[i], em_of[i] = em[:, 0, :], em[:, 1, :], em[:].rearrange("p a l -> p (a l)")
+
+        def mean_add(i, g):
+            if i not in em_of:
+                new_em(i)
+            nc.vector.tensor_tensor(
+                m_of[i][:, 512 * g : 512 * g + 512], mean_bank.pop((i, g))[:],
+                bias[kind_of(i), 1][:, 512 * g : 512 * g + 512], ALU.add)
+
+        def split(i):
+            return 2 if i in (0, N_TILES - 1) else 1
+
+        def kl_col(i):
+            return KL_COL[i // 4] + i % 4
+
+        def act_lv(i):
+            n = split(i)
+            w = L // n
+            if i not in em_of:
+                new_em(i)
+            for j in range(n):
+                c = slice(w * j, w * j + w)
+                nc.scalar.activation(th[i][:, c], th[i][:, c], ACTF.Tanh, scale=0.5,
+                                     accum_out=sums[0][:, j, kl_col(i) : kl_col(i) + 1])
+                nc.scalar.activation(e_of[i][:, c], th[i][:, c], ACTF.Exp)
+                if i == 0 and j == 0:
+                    group_w(("v", 1, 0, 0), "s")
+
+        def act_sq(i):
+            nc.scalar.activation(junk[:], em_of[i], ACTF.Square,
+                                 accum_out=sums[1][:, 0, kl_col(i) : kl_col(i) + 1])
+
+        def pool_en(i):
+            en_of[i] = sbt([P, L], F32, "en", 2)
+            for g in range(2):
+                c = slice(512 * g, 512 * g + 512)
+                nc.gpsimd.tensor_tensor(
+                    en_of[i][:, c].rearrange("p (t m) -> p t m", t=4),
+                    e_of[i][:, c].rearrange("p (t m) -> p t m", t=4),
+                    n_raw[i][:, c].rearrange("p (m t) -> p t m", t=4),
+                    ALU.mult)
+
+        def turn_z(i, g):
+            bk = bank("z")
+            for t in range(4):
+                lo = 512 * g + P * t
+                for part, src in enumerate((m_of[i], en_of[i])):
+                    nc.tensor.matmul(
+                        out=bk[:, P * t : P * t + P], lhsT=src[:, lo : lo + P], rhs=ident[:],
+                        start=(part == 0), stop=(part == 1),
+                        is_transpose=not (part == 0 and t % 2 == 0))
+            z_bank[i, g] = bk
+
+        def z_out(i, g):
+            b, s = divmod(i, 4)
+            if s == 0 and g == 0:
+                zbf[b] = sbt([P, 2, 2048], BF16, "zbf", 2)
+            row = 1 if BLOCKS[b] == "u" else 0
+            nc.vector.tensor_tensor(
+                zbf[b][:, g, 512 * s : 512 * s + 512].rearrange("p (r t) -> p r t", t=4),
+                z_bank.pop((i, g))[:].rearrange("p (t r) -> p r t", t=4),
+                gain[:, row, 4 * g : 4 * g + 4].unsqueeze(1).to_broadcast([P, P, 4]),
+                ALU.mult)
+
+        def quant_z(b, g, s0, n):
+            codes, scales = zq[b]
+            nc.vector.quantize_mx(
+                out=codes[:, g, P * s0 : P * (s0 + n)].bitcast(FP8X4),
+                scales=scales[:, g, P * s0 : P * (s0 + n)],
+                in_=zbf[b][:, g, 512 * s0 : 512 * (s0 + n)],
+            )
+
+        def make_bias(q, key, engine, tag="z"):
+            t = sbt([P, L], BF16, "bias%d" % q)
+            for g in range(2):
+                bk = bank(tag)
+                nc.tensor.matmul(out=bk[:], lhsT=sel[:, q, :], rhs=vecs[:, 512 * g : 512 * g + 512],
+                                 start=True, stop=True)
+                dst = t[:, 512 * g : 512 * g + 512].rearrange("p (t m) -> p t m", t=4)
+                src = bk[:].rearrange("p (m t) -> p t m", t=4)
+                if engine == "s":
+                    nc.scalar.copy(out=dst, in_=src)
+                else:
+                    nc.vector.tensor_copy(out=dst, in_=src)
+            bias[key] = t
 
         turn_x(0, 0, "xt")
-        turn_x(0, 1, "nt")
-        pb = bank("kl")
+        turn_x(0, 1, "dec")
+        copy_x(0, 0, "s")
+        copy_x(0, 1, "s")
+        make_bias(0, ("v", 0), "s")
+        make_bias(1, ("v", 1), "s", "mean")
+        group_w(("v", 0, 0, 0), "v")
+        group_w(("v", 0, 0, 1), "p")
+        quant_x(0)
+        pb = bank("xt")
         vw = vecs[:].bitcast(F32)
         for a in range(4):
             lo = 256 * (a // 2)
-            nc.tensor.transpose(pb[:, 128 * a : 128 * a + 128], vw[:, lo + a % 2 : lo + 256 : 2], ident[:])
-        curf = sbt([P, P], F32, "curf")
-        cb = bank("dec")
-
-        copy_x(0, 0, "s")
-        copy_x(0, 1, "s")
-        group_w(("v", 0, 0, 0), "v")
-        nc.vector.tensor_copy(out=curf[:], in_=cur[:])
-        nc.tensor.transpose(cb[:, 0:128], curf[:], ident[:])
+            nc.tensor.transpose(pb[:, P * a : P * a + P], vw[:, lo + a % 2 : lo + 256 : 2], ident[:])
         quant_w(("v", 0, 0, 0))
-        quant_x(0)
-        par = sbt([P, 6, 8], F32, "par")
+        gain = sbt([P, 2, 8], F32, "gain")
         nc.vector.tensor_copy(
-            out=par[:].rearrange("p r (a e) -> p r a e", e=2),
-            in_=pb[:].bitcast(BF16).rearrange("p (a r e) -> p r a e", a=4, e=2)[:, 0:6],
+            out=gain[:].rearrange("p r (a e) -> p r a e", e=2),
+            in_=pb[:].bitcast(BF16).rearrange("p (a r e) -> p r a e", a=4, e=2)[:, 1:3],
         )
-        group_w(("v", 1, 0, 0), "v")
-        nhb = sbt([P, 2, 8], F32, "nhb")
-        rb = sbt([P, 2, 8], F32, "rb")
-        for i in range(2):
-            nc.vector.tensor_scalar(nhb[:, i, :], par[:, 3 * i + 1, :], -0.5, None, ALU.mult)
-            nc.vector.tensor_scalar(rb[:, i, :], par[:, 3 * i, :], R2, None, ALU.mult)
-        nln2 = sbt([P, 1], F32, "nln2")
-        nc.vector.tensor_scalar(nln2[:], zero1[:], -math.log(2.0), None, ALU.add)
-        quant_w(("v", 1, 0, 0))
-        hcu = sbt([P, 4], F32, "hcu")
-        nc.vector.tensor_scalar(hcu[:], cb[:, 0:4], 0.5, None, ALU.mult)
-        load_u_chunk(1)
-        load_u_chunk(2)
-        load_x((2, 1), xu, 0, 512)
+        emit_lv(0, 0)
+        emit_lv(1, 0)
+        lv_add(0, 0)
+        quant_w(("v", 0, 0, 1))
+        lv_add(1, 0)
+        emit_lv(0, 1)
+        emit_lv(1, 1)
+        lv_add(0, 1)
+        group_w(("v", 1, 0, 1), "p")
+        lv_add(1, 1)
+        for i in range(1, 5):
+            load_u_chunk(i)
+        load_x((3, 0), xu, 0, 0)
 
-        emit_lv(0)
-        emit_noise(0)
-        emit_mean(0)
+        dec_bank, logit = {}, {}
 
-        nth, hm2, he2, zz, zbf = {}, {}, {}, {}, {}
-        red = sbt([P, 2, 20], F32, "red")
-        kl_bank = {}
-
-        def emit_kl(h, s):
-            if s == 0:
-                kl_bank[h] = bank("kl")
-            n = 0
-            for part in (nth[h], hm2[h], he2[h]):
-                for t in range(4):
-                    nc.tensor.matmul(
-                        out=kl_bank[h][:, 128 * s : 128 * s + 128],
-                        lhsT=part[:, t, 128 * s : 128 * s + 128],
-                        rhs=ident[:],
-                        start=(n == 0),
-                        stop=(n == 11),
-                        is_transpose=True,
-                    )
-                    n += 1
-
-        def reduce_kl(h):
-            b, g = divmod(h, 2)
-            j = KL_COL[b]
-            nc.vector.tensor_reduce(
-                out=red[:, g, j : j + 4],
-                in_=kl_bank.pop(h)[:].rearrange("p (s c) -> p s c", s=4),
-                axis=AX.X,
-                op=ALU.add,
-            )
-
-        def gain_of(h):
-            b, g = divmod(h, 2)
-            row = 2 if BLOCKS[b] == "u" else 5
-            return par[:, row, 4 * g : 4 * g + 4].unsqueeze(1)
-
-        def quant_z(h, w0=0, w1=512):
-            b, g = divmod(h, 2)
-            codes, scales = zq[b]
-            nc.vector.quantize_mx(
-                out=codes[:, g, w0:w1].bitcast(FP8X4),
-                scales=scales[:, g, w0:w1],
-                in_=zbf[h][:, 4 * w0 : 4 * w1],
-            )
-
-        dec_bank = {}
-
-        def emit_dec(b, i, tag, bufs=1):
-            bk = bank(tag, bufs)
+        def emit_dec(b, i, tag):
+            bk = bank(tag)
             for g in range(2):
                 nc.tensor.matmul_mx(
                     out=bk[:],
-                    lhsT=zq[2][0][:, g, 128 * i : 128 * i + 128].bitcast(FP8X4),
-                    lhsT_scale=zq[2][1][:, g, 128 * i : 128 * i + 128],
+                    lhsT=zq[U_BLOCK][0][:, g, P * i : P * i + P].bitcast(FP8X4),
+                    lhsT_scale=zq[U_BLOCK][1][:, g, P * i : P * i + P],
                     rhs=zq[b][0][:, g, :].bitcast(FP8X4),
                     rhs_scale=zq[b][1][:, g, :],
                     start=(g == 0),
@@ -315,30 +361,28 @@ def tile_variational_link_decoder_f5_kernel(
                 )
             dec_bank[b, i] = bk
 
-        logit = {}
-
         def dec_add(b, i):
-            t = sbt([P, 512], F32, "logit", 5)
+            t = sbt([P, 512], F32, "logit", 7)
             v0 = 512 * V_INDEX[b]
             nc.vector.scalar_tensor_tensor(
                 t[:], dec_bank.pop((b, i))[:], 1.0 / math.sqrt(L), cvb[:, v0 : v0 + 512], ALU.mult, ALU.add)
             logit[b, i] = t
 
-        def dec_tanh(b, i):
-            t = logit[b, i]
-            nc.scalar.activation(t[:], t[:], ACTF.Tanh, bias=hcu[:, i : i + 1], scale=0.5)
-
         def dec_store(b, i):
             t = logit.pop((b, i))
             v0 = 512 * V_INDEX[b]
-            nc.gpsimd.tensor_scalar(t[:], t[:], 0.5, 0.5, ALU.mult, ALU.add)
-            nc.sync.dma_start(out=prob[128 * i : 128 * i + 128, v0 : v0 + 512], in_=t[:])
+            nc.scalar.activation(t[:], t[:], ACTF.Sigmoid, bias=cuc[:, i : i + 1], scale=1.0)
+            nc.sync.dma_start(out=prob[P * i : P * i + P, v0 : v0 + 512], in_=t[:])
 
-        pre = {p: [] for p in range(N_STEPS)}
-        pool_work = {p: [] for p in range(N_STEPS)}
-        x_work = {p: [] for p in range(N_STEPS)}
-        loads = {p: [] for p in range(N_STEPS)}
-        dec_work = {p: [] for p in range(N_STEPS)}
+        steps = range(N_TILES + 1)
+        pre = {p: [] for p in steps}
+        post = {p: [] for p in steps}
+        pool_work = {p: [] for p in steps}
+        mid_work = {p: [] for p in steps}
+        end_work = {p: [] for p in steps}
+        scalar_work = {p: [] for p in steps}
+        scalar_early = {p: [] for p in steps}
+        loads = {p: [] for p in steps}
 
         def later(table, p, func, *args):
             table[p].append((func, args))
@@ -347,144 +391,130 @@ def tile_variational_link_decoder_f5_kernel(
             for func, args in table[p]:
                 func(*args)
 
-        for m in range(2):
-            later(pre, m, group_w, ("v", m, 0, 1), "v")
-        for key, p in ((1, 0), ((2, 0), 2), ((2, 1), 4), (3, 7), (4, 10)):
-            later(x_work, p, turn_x, key, 0)
-            later(x_work, p + 1, turn_x, key, 1)
-            later(pre, p + 1, copy_x, key, 0, "v")
-            later(pre, p + 2, copy_x, key, 1, "v")
+        for p in range(3, N_TILES + 1, 2):
+            b, s = divmod(p - 3, 4)
+            for g in range(2):
+                later(pre, p, quant_z, b, g, s, 2)
+        x_steps = ((1, 0, "s"), (2, 3, "s"), ((3, 0), 5, "s"), ((3, 1), 7, "s"), (4, 11, "v"))
+        for key, p, engine in x_steps:
+            for half in range(2):
+                later(end_work, p, turn_x, key, half, ("xt", "dec")[half])
+                later(scalar_early, p + 1, copy_x, key, half, engine)
+            later(post, p + 1, quant_x, key)
         for i in range(8):
-            if i % 2:
-                later(pre, i + 1, group_w, u_chunks[i], "v")
-            else:
-                later(pool_work, i + 1, group_w, u_chunks[i], "p")
-        for m in range(2):
-            later(pre, m, quant_w, ("v", m, 0, 1))
-        for h in range(2 * N_BLOCKS - 1):
-            later(pre, 2 * h + 3, quant_z, h)
-        for i in range(8):
-            later(pre, i + 2, quant_w, u_chunks[i])
-        for key, p in ((1, 0), ((2, 0), 2), ((2, 1), 4), (3, 7), (4, 10)):
-            later(pre, p + 2, quant_x, key)
-        later(loads, 0, load_noise, 4)
-        later(loads, 0, load_u_chunk, 3)
-        later(loads, 1, load_u_chunk, 4)
-        later(loads, 1, load_u_chunk, 5)
-        later(loads, 2, load_u_chunk, 6)
-        later(loads, 2, load_noise, 5)
-        later(loads, 3, load_u_chunk, 7)
-        later(loads, 3, load_x, 3, xv, 1024, 0)
-        later(loads, 4, load_noise, 6)
-        later(loads, 5, load_x, 4, xv, 1536, 0)
-        later(loads, 6, load_noise, 7)
-        later(loads, 8, load_noise, 8)
-        later(loads, 10, load_noise, 9)
+            p = (1, 2, 3, 4, 5, 6, 7, 8)[i]
+            later(pool_work, p, group_w, u_chunks[i], "p")
+            later(post, p + 1, quant_w, u_chunks[i])
+        later(end_work, 6, make_bias, 2, ("u", 0), "v")
+        later(end_work, 8, make_bias, 3, ("u", 1), "v")
+        for i in range(6, N_TILES):
+            later(loads, i - 6, load_noise, i)
+        for i in (5, 6, 7):
+            later(loads, i - 4, load_u_chunk, i)
+        later(loads, 2, load_x, (3, 1), xu, 0, 512)
+        later(loads, 4, load_x, 4, xv, 1536, 0)
 
-        dec_list = {}
-        for n, (b, i) in enumerate([(b, i) for b in (0, 1, 3) for i in range(4)]):
-            p = 13 + n // 2
-            dec_list.setdefault(p, []).append((b, i))
-            later(dec_work, p, emit_dec, b, i, "xt" if n % 2 else "dec")
-            later(pre, p + 1, dec_add, b, i)
+        dec_tiles = [(b, i) for b in (0, 1, 2, 4) for i in range(4)]
+        early = dec_tiles[:6]
+        for n, (b, i) in enumerate(early):
+            p = 17 + n // 2
+            later(mid_work, p, emit_dec, b, i, "xt" if n % 2 else "dec")
+            later(post, p, dec_add, b, i)
 
-        for p in range(N_STEPS):
-            h, u = divmod(p, 2)
-            b, g = divmod(h, 2)
-            kind = 0 if BLOCKS[b] == "u" else 1
-            if u == 0:
-                nth[h] = sbt([P, 4, 512], F32, "nth", 2)
-                hm2[h] = sbt([P, 4, 512], F32, "hm2", 2)
-                he2[h] = sbt([P, 4, 512], F32, "he2", 2)
-                zz[h] = sbt([P, 4, 512], F32, "zz", 2)
-            for k in range(2):
-                t = 2 * u + k
-                c = 4 * g + t
-                nc.scalar.activation(
-                    nth[h][:, t, :], lv_bank.pop((p, k))[:], ACTF.Tanh,
-                    bias=nhb[:, kind, c : c + 1], scale=-0.5)
-            pair = nth[h][:, 2 * u : 2 * u + 2, :].rearrange("p k w -> p (k w)")
-            e = sbt([P, 2, 512], F32, "e", 2)
-            nc.scalar.activation(e[:].rearrange("p k w -> p (k w)"), pair, ACTF.Exp, scale=-1.0)
+        cuc = sbt([P, 4], F32, "cuc")
 
+        def make_cuc():
+            curf = sbt([P, P], F32, "curf")
+            nc.vector.tensor_copy(out=curf[:], in_=cur[:])
+            cb = bank("dec")
+            nc.tensor.transpose(cb[:, 0:P], curf[:], ident[:])
+            nc.vector.tensor_copy(out=cuc[:], in_=cb[:, 0:4])
+
+        def first_means():
+            for g in range(2):
+                quant_w(("v", 1, 0, g))
+                emit_mean(0, g)
+            for g in range(2):
+                mean_add(0, g)
+            for g in range(2):
+                emit_mean(1, g)
+
+        later(pre, 0, first_means)
+        later(post, 14, make_cuc)
+        for p in range(N_TILES):
+            act_lv(p)
+            pool_en(p)
             run(pool_work, p)
             run(pre, p)
-            if p + 1 < N_STEPS:
-                emit_lv(p + 1)
-            if h >= 1:
-                emit_kl(h - 1, 2 * u)
-                emit_kl(h - 1, 2 * u + 1)
-            run(x_work, p)
-
-            for k in range(2):
-                t = 2 * u + k
-                c = 4 * g + t
-                nc.scalar.activation(
-                    hm2[h][:, t, :], mean_bank[p, k][:], ACTF.Square,
-                    bias=rb[:, kind, c : c + 1], scale=R2)
-            for b2, i2 in dec_list.get(p - 1, []):
-                dec_tanh(b2, i2)
-                dec_store(b2, i2)
-            nc.scalar.activation(
-                he2[h][:, 2 * u : 2 * u + 2, :].rearrange("p k w -> p (k w)"), pair, ACTF.Exp,
-                bias=nln2[:], scale=-2.0)
-
-            nview = noise_bank.pop(p)[:].bitcast(BF16).rearrange("p (r e) -> p r e", e=2)
-            for k in range(2):
-                nc.vector.tensor_tensor(e[:, k, :], e[:, k, :], nview[:, :, k], ALU.mult)
-            for k in range(2):
-                t = 2 * u + k
-                c = 4 * g + t
-                nc.vector.scalar_tensor_tensor(
-                    zz[h][:, t, :], mean_bank.pop((p, k))[:], par[:, 3 * kind, c : c + 1], e[:, k, :],
-                    ALU.add, ALU.add)
-            if u == 1 and h >= 1:
-                reduce_kl(h - 1)
-            if p + 1 < N_STEPS:
-                emit_noise(p + 1)
-                emit_mean(p + 1)
-            run(dec_work, p)
+            run(scalar_early, p)
+            if p >= 1:
+                for g in range(2):
+                    turn_z(p - 1, g)
+            if 1 < p + 1 < N_TILES:
+                for g in range(2):
+                    lv_add(p + 1, g)
+            if p + 2 < N_TILES:
+                for g in range(2):
+                    emit_lv(p + 2, g)
+            if p + 1 < N_TILES:
+                for g in range(2):
+                    mean_add(p + 1, g)
+            if p + 2 < N_TILES:
+                for g in range(2):
+                    emit_mean(p + 2, g)
+            if p >= 1:
+                act_sq(p - 1)
+            run(mid_work, p)
+            run(scalar_work, p)
+            if p >= 1:
+                for g in range(2):
+                    z_out(p - 1, g)
+            run(post, p)
+            run(end_work, p)
             run(loads, p)
             if p == 4:
                 nc.sync.dma_start(out=cvb[:], in_=cv.partition_broadcast(P))
-            if u == 1:
-                zbf[h] = sbt([P, 2048], BF16, "zbf", 2)
-                if p + 1 < N_STEPS:
-                    nc.gpsimd.tensor_tensor(
-                        zbf[h][:].rearrange("p (w t) -> p w t", t=4),
-                        zz[h][:].rearrange("p t w -> p w t"),
-                        gain_of(h).to_broadcast([P, 512, 4]),
-                        ALU.mult)
 
-        last = 2 * N_BLOCKS - 1
-        for half in range(2):
-            w0 = 256 * half
-            nc.vector.tensor_tensor(
-                zbf[last][:, 4 * w0 : 4 * w0 + 1024].rearrange("p (w t) -> p w t", t=4),
-                zz[last][:, :, w0 : w0 + 256].rearrange("p t w -> p w t"),
-                gain_of(last).to_broadcast([P, 256, 4]),
-                ALU.mult)
-        quant_z(last, 0, 256)
-        quant_z(last, 256, 512)
-        for s in range(3):
-            emit_kl(last, s)
-        tail_tags = (("dec", 1), ("xt", 1), ("lv", 2), ("lv", 2))
-        for i in range(4):
-            emit_dec(4, i, tail_tags[i][0], tail_tags[i][1])
-        emit_kl(last, 3)
-        for i in range(4):
-            dec_add(4, i)
-            dec_tanh(4, i)
-            dec_store(4, i)
-        reduce_kl(last)
+        last = N_TILES - 1
+        rest = dec_tiles[6:]
+        tags = ("dec", "xt", "lv", "lv", "mean", "mean", "dec", "xt", "lv", "lv")
+        for g in range(2):
+            turn_z(last, g)
+            if g == 0:
+                for n in range(2):
+                    emit_dec(*rest[n], tags[n])
+        act_sq(last)
+        for b, i in early:
+            dec_store(b, i)
+        for n in range(2, 6):
+            emit_dec(*rest[n], tags[n])
+        for n in range(2):
+            dec_add(*rest[n])
+            z_out(last, n)
+        for g in range(2):
+            quant_z(4, g, 2, 2)
+        for n in range(2):
+            dec_store(*rest[n])
+        for n in range(2, 6):
+            dec_add(*rest[n])
+            dec_store(*rest[n])
+        for n in range(6, 10):
+            emit_dec(*rest[n], tags[n])
         klc = sbt([P, P], F32, "klc")
-        nc.vector.memset(klc[:], 0.0)
-        kls = sbt([P, 20], F32, "kls")
-        nc.vector.tensor_tensor(kls[:], red[:, 0, :], red[:, 1, :], ALU.add)
-        nc.vector.tensor_scalar(klc[:, 0:20], kls[:], 1.0 / L, -0.5, ALU.mult, ALU.add)
-        kb = bank("nt")
-        nc.tensor.transpose(kb[:, 0:128], klc[:], ident[:])
-        klt = sbt([P, P], F32, "klt")
-        nc.vector.tensor_copy(out=klt[:], in_=kb[:, 0:128])
-        nc.sync.dma_start(out=kl_u.rearrange("(j r) -> j r", r=P), in_=klt[0:4, :])
-        nc.sync.dma_start(out=kl_v.rearrange("(j r) -> j r", r=P), in_=klt[4:20, :])
+        nc.gpsimd.memset(klc[:], 0.0)
+        kls = sbt([P, 2, N_TILES], F32, "kls")
+        for n in range(2):
+            nc.vector.tensor_tensor(kls[:, n, :], sums[n][:, 0, :], sums[n][:, 1, :], ALU.add)
+        nc.vector.tensor_scalar(kls[:, 1, :], kls[:, 1, :], 0.5, None, ALU.mult)
+        nc.vector.tensor_tensor(kls[:, 1, :], kls[:, 1, :], kls[:, 0, :], ALU.subtract)
+        nc.vector.tensor_scalar(klc[:, 0:N_TILES], kls[:, 1, :], 1.0 / L, -0.5, ALU.mult, ALU.add)
+        kb = bank("mean")
+        nc.tensor.transpose(kb[:, 0:P], klc[:], ident[:])
+        for n in range(6, 10):
+            dec_add(*rest[n])
+            dec_store(*rest[n])
+            if n == 6:
+                klt = sbt([P, P], F32, "klt")
+                nc.vector.tensor_copy(out=klt[:], in_=kb[:, 0:P])
+                nc.sync.dma_start(out=kl_u.rearrange("(j r) -> j r", r=P), in_=klt[0:4, :])
+                nc.sync.dma_start(out=kl_v.rearrange("(j r) -> j r", r=P), in_=klt[4:20, :])

@@ -24,6 +24,7 @@ BLOCKS = ("v", "v", "v", "u", "v")
 V_INDEX = (0, 1, 2, 0, 3)
 KL_COL = (4, 8, 12, 0, 16)
 U_BLOCK = 3
+VEC_EN = tuple((i, g) for i in range(20) for g in range(2) if g == 1 and i % 3 != 0)
 
 
 def tile_variational_link_decoder_f5_kernel(
@@ -74,7 +75,7 @@ def tile_variational_link_decoder_f5_kernel(
             x_raw[key] = raw
 
         def load_w(key, source, c, g):
-            raw = sbt([P, 4, 512], BF16, "w_raw", 5)
+            raw = sbt([P, 4, 512], BF16, "w_raw", 4)
             nc.sync.dma_start(
                 out=raw[:],
                 in_=source[512 * c : 512 * c + 512, 512 * g : 512 * g + 512].rearrange("(p j) c -> p j c", j=4),
@@ -104,7 +105,6 @@ def tile_variational_link_decoder_f5_kernel(
         load_w(("v", 1, 0, 1), wv_mean, 0, 1)
         load_noise(1)
         load_x(1, xv, 512, 0)
-        load_u_chunk(0)
         load_noise(2)
         load_noise(3)
         load_x(2, xv, 1024, 0)
@@ -132,7 +132,7 @@ def tile_variational_link_decoder_f5_kernel(
 
         def group_w(key, engine):
             raw = w_raw.pop(key)
-            t = sbt([P, 2048], BF16, "grp", 4)
+            t = sbt([P, 2048], BF16, "grp", 5)
             dst = t[:].rearrange("p (t m j) -> p t m j", t=4, j=4)
             src = raw[:].rearrange("p j (m t) -> p t m j", t=4)
             if engine == "v":
@@ -166,7 +166,7 @@ def tile_variational_link_decoder_f5_kernel(
 
         def copy_x(key, half, engine):
             if half == 0:
-                grp[key] = sbt([P, 2048], BF16, "grp", 4)
+                grp[key] = sbt([P, 2048], BF16, "grp", 5)
             dst = grp[key][:].bitcast(F32)[:, 512 * half : 512 * half + 512].rearrange(
                 "p (s r w) -> p s r w", s=2, w=2)
             src = x_bank.pop((key, half))[:].rearrange("p (s w r) -> p s r w", s=2, w=2)
@@ -250,22 +250,23 @@ def tile_variational_link_decoder_f5_kernel(
                 nc.scalar.activation(th[i][:, c], th[i][:, c], ACTF.Tanh, scale=0.5,
                                      accum_out=sums[0][:, j, kl_col(i) : kl_col(i) + 1])
                 nc.scalar.activation(e_of[i][:, c], th[i][:, c], ACTF.Exp)
-                if i == 0 and j == 0:
-                    group_w(("v", 1, 0, 0), "s")
 
         def act_sq(i):
             nc.scalar.activation(junk[:], em_of[i], ACTF.Square,
                                  accum_out=sums[1][:, 0, kl_col(i) : kl_col(i) + 1])
 
-        def pool_en(i):
-            en_of[i] = sbt([P, L], F32, "en", 2)
-            for g in range(2):
-                c = slice(512 * g, 512 * g + 512)
-                nc.gpsimd.tensor_tensor(
-                    en_of[i][:, c].rearrange("p (t m) -> p t m", t=4),
-                    e_of[i][:, c].rearrange("p (t m) -> p t m", t=4),
-                    n_raw[i][:, c].rearrange("p (m t) -> p t m", t=4),
-                    ALU.mult)
+        def noise_product(engine, i, g):
+            if i not in en_of:
+                en_of[i] = sbt([P, L], F32, "en", 2)
+            c = slice(512 * g, 512 * g + 512)
+            engine.tensor_tensor(
+                en_of[i][:, c].rearrange("p (t c m) -> p c t m", t=4, m=4),
+                e_of[i][:, c].rearrange("p (t c m) -> p c t m", t=4, m=4),
+                n_raw[i][:, c].rearrange("p (c m t) -> p c t m", t=4, m=4),
+                ALU.mult)
+
+        def en_on_vector(i, g):
+            return (i, g) in VEC_EN
 
         def turn_z(i, g):
             bk = bank("z")
@@ -318,7 +319,9 @@ def tile_variational_link_decoder_f5_kernel(
         make_bias(0, ("v", 0), "s")
         make_bias(1, ("v", 1), "s", "mean")
         group_w(("v", 0, 0, 0), "v")
-        group_w(("v", 0, 0, 1), "p")
+        group_w(("v", 1, 0, 0), "p")
+        group_w(("v", 1, 0, 1), "p")
+        group_w(("v", 0, 0, 1), "v")
         quant_x(0)
         pb = bank("xt")
         vw = vecs[:].bitcast(F32)
@@ -332,16 +335,17 @@ def tile_variational_link_decoder_f5_kernel(
             in_=pb[:].bitcast(BF16).rearrange("p (a r e) -> p r a e", a=4, e=2)[:, 1:3],
         )
         emit_lv(0, 0)
-        emit_lv(1, 0)
-        lv_add(0, 0)
         quant_w(("v", 0, 0, 1))
-        lv_add(1, 0)
         emit_lv(0, 1)
-        emit_lv(1, 1)
+        lv_add(0, 0)
         lv_add(0, 1)
-        group_w(("v", 1, 0, 1), "p")
+        emit_lv(1, 0)
+        emit_lv(1, 1)
+        lv_add(1, 0)
         lv_add(1, 1)
-        for i in range(1, 5):
+        turn_x(1, 0, "xt")
+        turn_x(1, 1, "dec")
+        for i in range(2):
             load_u_chunk(i)
         load_x((3, 0), xu, 0, 0)
 
@@ -361,18 +365,19 @@ def tile_variational_link_decoder_f5_kernel(
                 )
             dec_bank[b, i] = bk
 
-        def dec_add(b, i):
-            t = sbt([P, 512], F32, "logit", 7)
+        def dec_add(b, i, t=None):
+            if t is None:
+                t = sbt([P, 512], F32, "logit", 6)[:]
             v0 = 512 * V_INDEX[b]
             nc.vector.scalar_tensor_tensor(
-                t[:], dec_bank.pop((b, i))[:], 1.0 / math.sqrt(L), cvb[:, v0 : v0 + 512], ALU.mult, ALU.add)
+                t, dec_bank.pop((b, i))[:], 1.0 / math.sqrt(L), cvb[:, v0 : v0 + 512], ALU.mult, ALU.add)
             logit[b, i] = t
 
         def dec_store(b, i):
             t = logit.pop((b, i))
             v0 = 512 * V_INDEX[b]
-            nc.scalar.activation(t[:], t[:], ACTF.Sigmoid, bias=cuc[:, i : i + 1], scale=1.0)
-            nc.sync.dma_start(out=prob[P * i : P * i + P, v0 : v0 + 512], in_=t[:])
+            nc.scalar.activation(t, t, ACTF.Sigmoid, bias=cuc[:, i : i + 1], scale=1.0)
+            nc.sync.dma_start(out=prob[P * i : P * i + P, v0 : v0 + 512], in_=t)
 
         steps = range(N_TILES + 1)
         pre = {p: [] for p in steps}
@@ -391,11 +396,14 @@ def tile_variational_link_decoder_f5_kernel(
             for func, args in table[p]:
                 func(*args)
 
-        for p in range(3, N_TILES + 1, 2):
-            b, s = divmod(p - 3, 4)
+        for p in range(2, N_TILES, 2):
+            b, s = divmod(p - 2, 4)
             for g in range(2):
-                later(pre, p, quant_z, b, g, s, 2)
-        x_steps = ((1, 0, "s"), (2, 3, "s"), ((3, 0), 5, "s"), ((3, 1), 7, "s"), (4, 11, "v"))
+                later(post, p, quant_z, b, g, s, 2)
+        for half in range(2):
+            later(scalar_early, 0, copy_x, 1, half, "s")
+        later(post, 0, quant_x, 1)
+        x_steps = ((2, 3, "s"), ((3, 0), 5, "s"), ((3, 1), 7, "s"), (4, 11, "v"))
         for key, p, engine in x_steps:
             for half in range(2):
                 later(end_work, p, turn_x, key, half, ("xt", "dec")[half])
@@ -409,8 +417,8 @@ def tile_variational_link_decoder_f5_kernel(
         later(end_work, 8, make_bias, 3, ("u", 1), "v")
         for i in range(6, N_TILES):
             later(loads, i - 6, load_noise, i)
-        for i in (5, 6, 7):
-            later(loads, i - 4, load_u_chunk, i)
+        for i, p in ((2, 0), (3, 0), (4, 1), (5, 2), (6, 3), (7, 4)):
+            later(loads, p, load_u_chunk, i)
         later(loads, 2, load_x, (3, 1), xu, 0, 512)
         later(loads, 4, load_x, 4, xv, 1536, 0)
 
@@ -443,7 +451,9 @@ def tile_variational_link_decoder_f5_kernel(
         later(post, 14, make_cuc)
         for p in range(N_TILES):
             act_lv(p)
-            pool_en(p)
+            for g in range(2):
+                if not en_on_vector(p, g):
+                    noise_product(nc.gpsimd, p, g)
             run(pool_work, p)
             run(pre, p)
             run(scalar_early, p)
@@ -469,6 +479,9 @@ def tile_variational_link_decoder_f5_kernel(
             if p >= 1:
                 for g in range(2):
                     z_out(p - 1, g)
+            for g in range(2):
+                if en_on_vector(p, g):
+                    noise_product(nc.vector, p, g)
             run(post, p)
             run(end_work, p)
             run(loads, p)
@@ -477,6 +490,10 @@ def tile_variational_link_decoder_f5_kernel(
 
         last = N_TILES - 1
         rest = dec_tiles[6:]
+        spare = []
+        for n in range(3):
+            em = sbt([P, 2, L], F32, "em", 4)
+            spare.extend(em[:, a, 512 * g : 512 * g + 512] for a in range(2) for g in range(2))
         tags = ("dec", "xt", "lv", "lv", "mean", "mean", "dec", "xt", "lv", "lv")
         for g in range(2):
             turn_z(last, g)
@@ -489,14 +506,14 @@ def tile_variational_link_decoder_f5_kernel(
         for n in range(2, 6):
             emit_dec(*rest[n], tags[n])
         for n in range(2):
-            dec_add(*rest[n])
+            dec_add(*rest[n], spare[n])
             z_out(last, n)
         for g in range(2):
             quant_z(4, g, 2, 2)
         for n in range(2):
             dec_store(*rest[n])
         for n in range(2, 6):
-            dec_add(*rest[n])
+            dec_add(*rest[n], spare[n])
             dec_store(*rest[n])
         for n in range(6, 10):
             emit_dec(*rest[n], tags[n])
@@ -511,7 +528,7 @@ def tile_variational_link_decoder_f5_kernel(
         kb = bank("mean")
         nc.tensor.transpose(kb[:, 0:P], klc[:], ident[:])
         for n in range(6, 10):
-            dec_add(*rest[n])
+            dec_add(*rest[n], spare[n])
             dec_store(*rest[n])
             if n == 6:
                 klt = sbt([P, P], F32, "klt")

@@ -24,7 +24,8 @@ BLOCKS = ("v", "v", "v", "u", "v")
 V_INDEX = (0, 1, 2, 0, 3)
 KL_COL = (4, 8, 12, 0, 16)
 U_BLOCK = 3
-VEC_EN = tuple((i, g) for i in range(20) for g in range(2) if g == 1 and i % 3 != 0)
+GRP_PIECE = 256
+VEC_EN = tuple((i, g) for i in range(20) for g in range(2) if g == 1 and i < 10)
 
 
 def tile_variational_link_decoder_f5_kernel(
@@ -133,15 +134,15 @@ def tile_variational_link_decoder_f5_kernel(
         def group_w(key, engine):
             raw = w_raw.pop(key)
             t = sbt([P, 2048], BF16, "grp", 5)
-            dst = t[:].rearrange("p (t m j) -> p t m j", t=4, j=4)
-            src = raw[:].rearrange("p j (m t) -> p t m j", t=4)
+            dst = t[:].rearrange("p (c j) -> p c j", j=4)
+            src = raw[:].rearrange("p j c -> p c j")
             if engine == "v":
                 nc.vector.tensor_copy(out=dst, in_=src)
             elif engine == "s":
                 nc.scalar.copy(out=dst, in_=src)
             else:
-                for t4 in range(4):
-                    nc.gpsimd.tensor_scalar(dst[:, t4], src[:, t4], 1.0, 0.0, ALU.mult, ALU.add)
+                for c0 in range(0, 512, GRP_PIECE):
+                    nc.gpsimd.tensor_scalar(dst[:, c0 : c0 + GRP_PIECE], src[:, c0 : c0 + GRP_PIECE], 1.0, 0.0, ALU.mult, ALU.add)
             grp[key] = t
 
         def quant_w(key):
@@ -220,8 +221,9 @@ def tile_variational_link_decoder_f5_kernel(
             if g == 0:
                 th[i] = sbt([P, L], F32, "th", 2)
             nc.vector.tensor_tensor(
-                th[i][:, 512 * g : 512 * g + 512], lv_bank.pop((i, g))[:],
-                bias[kind_of(i), 0][:, 512 * g : 512 * g + 512], ALU.add)
+                th[i][:, 512 * g : 512 * g + 512].rearrange("p (t m) -> p t m", t=4),
+                lv_bank.pop((i, g))[:].rearrange("p (m t) -> p t m", t=4),
+                bias[kind_of(i), 0][:, 512 * g : 512 * g + 512].rearrange("p (t m) -> p t m", t=4), ALU.add)
 
         def new_em(i):
             em = sbt([P, 2, L], F32, "em", 4)
@@ -231,8 +233,9 @@ def tile_variational_link_decoder_f5_kernel(
             if i not in em_of:
                 new_em(i)
             nc.vector.tensor_tensor(
-                m_of[i][:, 512 * g : 512 * g + 512], mean_bank.pop((i, g))[:],
-                bias[kind_of(i), 1][:, 512 * g : 512 * g + 512], ALU.add)
+                m_of[i][:, 512 * g : 512 * g + 512].rearrange("p (t m) -> p t m", t=4),
+                mean_bank.pop((i, g))[:].rearrange("p (m t) -> p t m", t=4),
+                bias[kind_of(i), 1][:, 512 * g : 512 * g + 512].rearrange("p (t m) -> p t m", t=4), ALU.add)
 
         def split(i):
             return 2 if i in (0, N_TILES - 1) else 1
@@ -276,7 +279,7 @@ def tile_variational_link_decoder_f5_kernel(
                     nc.tensor.matmul(
                         out=bk[:, P * t : P * t + P], lhsT=src[:, lo : lo + P], rhs=ident[:],
                         start=(part == 0), stop=(part == 1),
-                        is_transpose=not (part == 0 and t % 2 == 0))
+                        is_transpose=not (part == 0 and t == 0))
             z_bank[i, g] = bk
 
         def z_out(i, g):
@@ -500,7 +503,6 @@ def tile_variational_link_decoder_f5_kernel(
             if g == 0:
                 for n in range(2):
                     emit_dec(*rest[n], tags[n])
-        act_sq(last)
         for b, i in early:
             dec_store(b, i)
         for n in range(2, 6):
@@ -512,6 +514,7 @@ def tile_variational_link_decoder_f5_kernel(
             quant_z(4, g, 2, 2)
         for n in range(2):
             dec_store(*rest[n])
+        act_sq(last)
         for n in range(2, 6):
             dec_add(*rest[n], spare[n])
             dec_store(*rest[n])
@@ -519,6 +522,9 @@ def tile_variational_link_decoder_f5_kernel(
             emit_dec(*rest[n], tags[n])
         klc = sbt([P, P], F32, "klc")
         nc.gpsimd.memset(klc[:], 0.0)
+        for n in range(6, 10):
+            dec_add(*rest[n], spare[n])
+            dec_store(*rest[n])
         kls = sbt([P, 2, N_TILES], F32, "kls")
         for n in range(2):
             nc.vector.tensor_tensor(kls[:, n, :], sums[n][:, 0, :], sums[n][:, 1, :], ALU.add)
@@ -527,11 +533,7 @@ def tile_variational_link_decoder_f5_kernel(
         nc.vector.tensor_scalar(klc[:, 0:N_TILES], kls[:, 1, :], 1.0 / L, -0.5, ALU.mult, ALU.add)
         kb = bank("mean")
         nc.tensor.transpose(kb[:, 0:P], klc[:], ident[:])
-        for n in range(6, 10):
-            dec_add(*rest[n], spare[n])
-            dec_store(*rest[n])
-            if n == 6:
-                klt = sbt([P, P], F32, "klt")
-                nc.vector.tensor_copy(out=klt[:], in_=kb[:, 0:P])
-                nc.sync.dma_start(out=kl_u.rearrange("(j r) -> j r", r=P), in_=klt[0:4, :])
-                nc.sync.dma_start(out=kl_v.rearrange("(j r) -> j r", r=P), in_=klt[4:20, :])
+        klt = sbt([P, P], F32, "klt")
+        nc.vector.tensor_copy(out=klt[:], in_=kb[:, 0:P])
+        nc.sync.dma_start(out=kl_u.rearrange("(j r) -> j r", r=P), in_=klt[0:4, :])
+        nc.sync.dma_start(out=kl_v.rearrange("(j r) -> j r", r=P), in_=klt[4:20, :])

import math
from contextlib import ExitStack

import concourse.mybir as mybir
from concourse.masks import make_identity

U, V, KU, KV, L = 512, 2048, 1024, 512, 1024
FLOPS = 2 * (2 * U * KU * L + 2 * V * KV * L + U * V * L)

F32 = mybir.dt.float32
BF16 = mybir.dt.bfloat16
U32 = mybir.dt.uint32
U8 = mybir.dt.uint8
FP8X4 = mybir.dt.float8_e4m3fn_x4
ALU = mybir.AluOpType
ACTF = mybir.ActivationFunctionType
AX = mybir.AxisListType

P = 128
ROWS = 512
N_BLOCKS = 5
N_TILES = 4 * N_BLOCKS
BLOCKS = ("v", "v", "v", "u", "v")
V_INDEX = (0, 1, 2, 0, 3)
KL_COL = (4, 8, 12, 0, 16)
U_BLOCK = 3
GRP_PIECE = 256
VEC_EN = tuple((i, g) for i in range(20) for g in range(2) if g == 1 and i < 10)


def tile_variational_link_decoder_f5_kernel(
    tc, xu, wu_mean, wu_lv, bu_mean, bu_lv, noise_u, gain_u,
    xv, wv_mean, wv_lv, bv_mean, bv_lv, noise_v, gain_v, cu, cv,
    prob, kl_u, kl_v,
):
    nc = tc.nc
    with ExitStack() as ctx:
        sb = ctx.enter_context(tc.tile_pool(name="sb", bufs=1))
        ps = ctx.enter_context(tc.psum_pool(name="ps", bufs=1))
        ctx.enter_context(tc.manual_schedule())

        def sbt(shape, dt, tag, bufs=1):
            return sb.tile(shape, dt, name=tag, tag=tag, bufs=bufs, align_bytes=64)

        BANKS = {"lv": 2, "mean": 2, "z": 2, "xt": 1, "dec": 1}

        def bank(tag):
            return ps.tile([P, 512], F32, name=tag, tag=tag, bufs=BANKS[tag])

        zero1 = sbt([P, 1], F32, "zero1")
        nc.vector.memset(zero1[:], 0.0)
        vecs = sbt([P, L], BF16, "vecs")
        nc.vector.memset(vecs[:], 0.0)
        cur = sbt([P, P], BF16, "cur")
        nc.vector.memset(cur[:], 0.0)
        dummy = sbt([P, 1], F32, "dummy")
        nc.scalar.activation(dummy[:], zero1[:], ACTF.Exp)
        sel = sbt([P, 4, P], BF16, "sel")
        nc.vector.memset(sel[:], 0.0)
        for q in range(4):
            nc.vector.memset(sel[32 * q : 32 * q + 1, q, :], 1.0)
        sums = [sbt([P, 2, N_TILES], F32, "sum_%s" % name) for name in ("th", "sq")]
        for t in sums:
            nc.vector.memset(t[:], 0.0)

        x_raw, w_raw, n_raw = {}, {}, {}

        def load_x(key, source, row0, col0):
            raw = sbt([P, 4, 512], BF16, "x_raw", 3)
            for half in range(2):
                r0 = row0 + 256 * half
                nc.sync.dma_start(
                    out=raw[:, 2 * half : 2 * half + 2, :],
                    in_=source[r0 : r0 + 256, col0 : col0 + 512].rearrange("(s p) k -> p s k", p=P),
                )
            x_raw[key] = raw

        def load_w(key, source, c, g):
            raw = sbt([P, 4, 512], BF16, "w_raw", 4)
            nc.sync.dma_start(
                out=raw[:],
                in_=source[512 * c : 512 * c + 512, 512 * g : 512 * g + 512].rearrange("(p j) c -> p j c", j=4),
            )
            w_raw[key] = raw

        def load_noise(i):
            b, s = divmod(i, 4)
            source = noise_u if BLOCKS[b] == "u" else noise_v
            r0 = ROWS * V_INDEX[b] + P * s
            raw = sbt([P, L], BF16, "n_raw", 6)
            nc.sync.dma_start(out=raw[:], in_=source[r0 : r0 + P, :])
            n_raw[i] = raw

        u_chunks = [("u", m, c, g) for m in range(2) for g in range(2) for c in range(2)]
        u_src = (wu_lv, wu_mean)

        def load_u_chunk(i):
            key = u_chunks[i]
            load_w(key, u_src[key[1]], key[2], key[3])

        load_x(0, xv, 0, 0)
        load_w(("v", 0, 0, 0), wv_lv, 0, 0)
        load_w(("v", 0, 0, 1), wv_lv, 0, 1)
        load_w(("v", 1, 0, 0), wv_mean, 0, 0)
        load_noise(0)
        load_w(("v", 1, 0, 1), wv_mean, 0, 1)
        load_noise(1)
        load_x(1, xv, 512, 0)
        load_noise(2)
        load_noise(3)
        load_x(2, xv, 1024, 0)
        load_noise(4)
        load_noise(5)

        for r, vec in ((0, bv_lv), (32, bv_mean), (1, gain_v), (64, bu_lv), (96, bu_mean), (2, gain_u)):
            nc.scalar.dma_start(out=vecs[r : r + 1, :], in_=vec.rearrange("(o l) -> o l", o=1))
        nc.scalar.dma_start(out=cur[0:4, :], in_=cu.rearrange("(i p) -> i p", p=P))
        cvb = sbt([P, V], BF16, "cvb")

        ident = sbt([P, P], F32, "ident")
        make_identity(nc, ident[:])

        wq = {
            "v": (sbt([P, 2, 1, L], U32, "wv_codes"), sbt([P, 2, 1, L], U8, "wv_scales")),
            "u": (sbt([P, 2, 2, L], U32, "wu_codes"), sbt([P, 2, 2, L], U8, "wu_scales")),
        }
        xq = {}
        zq = [
            (sbt([P, 2, 512], U32, "z_codes%d" % b), sbt([P, 2, 512], U8, "z_scales%d" % b))
            for b in range(N_BLOCKS)
        ]
        grp = {}

        def group_w(key, engine):
            raw = w_raw.pop(key)
            t = sbt([P, 2048], BF16, "grp", 5)
            dst = t[:].rearrange("p (c j) -> p c j", j=4)
            src = raw[:].rearrange("p j c -> p c j")
            if engine == "v":
                nc.vector.tensor_copy(out=dst, in_=src)
            elif engine == "s":
                nc.scalar.copy(out=dst, in_=src)
            else:
                for c0 in range(0, 512, GRP_PIECE):
                    nc.gpsimd.tensor_scalar(dst[:, c0 : c0 + GRP_PIECE], src[:, c0 : c0 + GRP_PIECE], 1.0, 0.0, ALU.mult, ALU.add)
            grp[key] = t

        def quant_w(key):
            kind, m, c, g = key
            codes, scales = wq[kind]
            nc.vector.quantize_mx(
                out=codes[:, m, c, 512 * g : 512 * g + 512].bitcast(FP8X4),
                scales=scales[:, m, c, 512 * g : 512 * g + 512],
                in_=grp.pop(key)[:],
            )

        x_bank = {}

        def turn_x(key, half, tag="xt"):
            words = x_raw[key][:].bitcast(F32)
            bk = bank(tag)
            for s in range(2):
                for w in range(2):
                    o = 256 * s + 128 * w
                    nc.tensor.transpose(bk[:, o : o + 128], words[:, 2 * half + s, w:256:2], ident[:])
            x_bank[key, half] = bk

        def copy_x(key, half, engine):
            if half == 0:
                grp[key] = sbt([P, 2048], BF16, "grp", 5)
            dst = grp[key][:].bitcast(F32)[:, 512 * half : 512 * half + 512].rearrange(
                "p (s r w) -> p s r w", s=2, w=2)
            src = x_bank.pop((key, half))[:].rearrange("p (s w r) -> p s r w", s=2, w=2)
            if engine == "v":
                nc.vector.tensor_copy(out=dst, in_=src)
            else:
                nc.scalar.copy(out=dst, in_=src)

        def quant_x(key):
            codes = sbt([P, 512], U32, "x_codes", 4)
            scales = sbt([P, 512], U8, "x_scales", 4)
            nc.vector.quantize_mx(out=codes[:].bitcast(FP8X4), scales=scales[:], in_=grp.pop(key)[:])
            xq[key] = (codes, scales)

        def stage1(bk, i, m, g):
            b, s = divmod(i, 4)
            kind = BLOCKS[b]
            codes, scales = wq[kind]
            n = 2 if kind == "u" else 1
            for c in range(n):
                xc, xs = xq[(b, c) if kind == "u" else b]
                nc.tensor.matmul_mx(
                    out=bk[:],
                    lhsT=xc[:, P * s : P * s + P].bitcast(FP8X4),
                    lhsT_scale=xs[:, P * s : P * s + P],
                    rhs=codes[:, m, c, 512 * g : 512 * g + 512].bitcast(FP8X4),
                    rhs_scale=scales[:, m, c, 512 * g : 512 * g + 512],
                    start=(c == 0),
                    stop=(c == n - 1),
                )

        lv_bank, mean_bank, z_bank = {}, {}, {}
        th, e_of, en_of, m_of, em_of, zbf = {}, {}, {}, {}, {}, {}
        junk = sbt([P, 2 * L], F32, "junk")
        bias = {}

        def kind_of(i):
            return BLOCKS[i // 4]

        def emit_lv(i, g):
            bk = bank("lv")
            stage1(bk, i, 0, g)
            lv_bank[i, g] = bk

        def emit_mean(i, g):
            bk = bank("mean")
            stage1(bk, i, 1, g)
            mean_bank[i, g] = bk

        def lv_add(i, g):
            if g == 0:
                th[i] = sbt([P, L], F32, "th", 2)
            nc.vector.tensor_tensor(
                th[i][:, 512 * g : 512 * g + 512].rearrange("p (t m) -> p t m", t=4),
                lv_bank.pop((i, g))[:].rearrange("p (m t) -> p t m", t=4),
                bias[kind_of(i), 0][:, 512 * g : 512 * g + 512].rearrange("p (t m) -> p t m", t=4), ALU.add)

        def new_em(i):
            em = sbt([P, 2, L], F32, "em", 4)
            e_of[i], m_of[i], em_of[i] = em[:, 0, :], em[:, 1, :], em[:].rearrange("p a l -> p (a l)")

        def mean_add(i, g):
            if i not in em_of:
                new_em(i)
            nc.vector.tensor_tensor(
                m_of[i][:, 512 * g : 512 * g + 512].rearrange("p (t m) -> p t m", t=4),
                mean_bank.pop((i, g))[:].rearrange("p (m t) -> p t m", t=4),
                bias[kind_of(i), 1][:, 512 * g : 512 * g + 512].rearrange("p (t m) -> p t m", t=4), ALU.add)

        def split(i):
            return 2 if i in (0, N_TILES - 1) else 1

        def kl_col(i):
            return KL_COL[i // 4] + i % 4

        def act_lv(i):
            n = split(i)
            w = L // n
            if i not in em_of:
                new_em(i)
            for j in range(n):
                c = slice(w * j, w * j + w)
                nc.scalar.activation(th[i][:, c], th[i][:, c], ACTF.Tanh, scale=0.5,
                                     accum_out=sums[0][:, j, kl_col(i) : kl_col(i) + 1])
                nc.scalar.activation(e_of[i][:, c], th[i][:, c], ACTF.Exp)

        def act_sq(i):
            nc.scalar.activation(junk[:], em_of[i], ACTF.Square,
                                 accum_out=sums[1][:, 0, kl_col(i) : kl_col(i) + 1])

        def noise_product(engine, i, g):
            if i not in en_of:
                en_of[i] = sbt([P, L], F32, "en", 2)
            c = slice(512 * g, 512 * g + 512)
            engine.tensor_tensor(
                en_of[i][:, c].rearrange("p (t c m) -> p c t m", t=4, m=4),
                e_of[i][:, c].rearrange("p (t c m) -> p c t m", t=4, m=4),
                n_raw[i][:, c].rearrange("p (c m t) -> p c t m", t=4, m=4),
                ALU.mult)

        def en_on_vector(i, g):
            return (i, g) in VEC_EN

        def turn_z(i, g):
            bk = bank("z")
            for t in range(4):
                lo = 512 * g + P * t
                for part, src in enumerate((m_of[i], en_of[i])):
                    nc.tensor.matmul(
                        out=bk[:, P * t : P * t + P], lhsT=src[:, lo : lo + P], rhs=ident[:],
                        start=(part == 0), stop=(part == 1),
                        is_transpose=not (part == 0 and t == 0))
            z_bank[i, g] = bk

        def z_out(i, g):
            b, s = divmod(i, 4)
            if s == 0 and g == 0:
                zbf[b] = sbt([P, 2, 2048], BF16, "zbf", 2)
            row = 1 if BLOCKS[b] == "u" else 0
            nc.vector.tensor_tensor(
                zbf[b][:, g, 512 * s : 512 * s + 512].rearrange("p (r t) -> p r t", t=4),
                z_bank.pop((i, g))[:].rearrange("p (t r) -> p r t", t=4),
                gain[:, row, 4 * g : 4 * g + 4].unsqueeze(1).to_broadcast([P, P, 4]),
                ALU.mult)

        def quant_z(b, g, s0, n):
            codes, scales = zq[b]
            nc.vector.quantize_mx(
                out=codes[:, g, P * s0 : P * (s0 + n)].bitcast(FP8X4),
                scales=scales[:, g, P * s0 : P * (s0 + n)],
                in_=zbf[b][:, g, 512 * s0 : 512 * (s0 + n)],
            )

        def make_bias(q, key, engine, tag="z"):
            t = sbt([P, L], BF16, "bias%d" % q)
            for g in range(2):
                bk = bank(tag)
                nc.tensor.matmul(out=bk[:], lhsT=sel[:, q, :], rhs=vecs[:, 512 * g : 512 * g + 512],
                                 start=True, stop=True)
                dst = t[:, 512 * g : 512 * g + 512].rearrange("p (t m) -> p t m", t=4)
                src = bk[:].rearrange("p (m t) -> p t m", t=4)
                if engine == "s":
                    nc.scalar.copy(out=dst, in_=src)
                else:
                    nc.vector.tensor_copy(out=dst, in_=src)
            bias[key] = t

        turn_x(0, 0, "xt")
        turn_x(0, 1, "dec")
        copy_x(0, 0, "s")
        copy_x(0, 1, "s")
        make_bias(0, ("v", 0), "s")
        make_bias(1, ("v", 1), "s", "mean")
        group_w(("v", 0, 0, 0), "v")
        group_w(("v", 1, 0, 0), "p")
        group_w(("v", 1, 0, 1), "p")
        group_w(("v", 0, 0, 1), "v")
        quant_x(0)
        pb = bank("xt")
        vw = vecs[:].bitcast(F32)
        for a in range(4):
            lo = 256 * (a // 2)
            nc.tensor.transpose(pb[:, P * a : P * a + P], vw[:, lo + a % 2 : lo + 256 : 2], ident[:])
        quant_w(("v", 0, 0, 0))
        gain = sbt([P, 2, 8], F32, "gain")
        nc.vector.tensor_copy(
            out=gain[:].rearrange("p r (a e) -> p r a e", e=2),
            in_=pb[:].bitcast(BF16).rearrange("p (a r e) -> p r a e", a=4, e=2)[:, 1:3],
        )
        emit_lv(0, 0)
        quant_w(("v", 0, 0, 1))
        emit_lv(0, 1)
        lv_add(0, 0)
        lv_add(0, 1)
        emit_lv(1, 0)
        emit_lv(1, 1)
        lv_add(1, 0)
        lv_add(1, 1)
        turn_x(1, 0, "xt")
        turn_x(1, 1, "dec")
        for i in range(2):
            load_u_chunk(i)
        load_x((3, 0), xu, 0, 0)

        dec_bank, logit = {}, {}

        def emit_dec(b, i, tag):
            bk = bank(tag)
            for g in range(2):
                nc.tensor.matmul_mx(
                    out=bk[:],
                    lhsT=zq[U_BLOCK][0][:, g, P * i : P * i + P].bitcast(FP8X4),
                    lhsT_scale=zq[U_BLOCK][1][:, g, P * i : P * i + P],
                    rhs=zq[b][0][:, g, :].bitcast(FP8X4),
                    rhs_scale=zq[b][1][:, g, :],
                    start=(g == 0),
                    stop=(g == 1),
                )
            dec_bank[b, i] = bk

        def dec_add(b, i, t=None):
            if t is None:
                t = sbt([P, 512], F32, "logit", 6)[:]
            v0 = 512 * V_INDEX[b]
            nc.vector.scalar_tensor_tensor(
                t, dec_bank.pop((b, i))[:], 1.0 / math.sqrt(L), cvb[:, v0 : v0 + 512], ALU.mult, ALU.add)
            logit[b, i] = t

        def dec_store(b, i):
            t = logit.pop((b, i))
            v0 = 512 * V_INDEX[b]
            nc.scalar.activation(t, t, ACTF.Sigmoid, bias=cuc[:, i : i + 1], scale=1.0)
            nc.sync.dma_start(out=prob[P * i : P * i + P, v0 : v0 + 512], in_=t)

        steps = range(N_TILES + 1)
        pre = {p: [] for p in steps}
        post = {p: [] for p in steps}
        pool_work = {p: [] for p in steps}
        mid_work = {p: [] for p in steps}
        end_work = {p: [] for p in steps}
        scalar_work = {p: [] for p in steps}
        scalar_early = {p: [] for p in steps}
        loads = {p: [] for p in steps}

        def later(table, p, func, *args):
            table[p].append((func, args))

        def run(table, p):
            for func, args in table[p]:
                func(*args)

        for p in range(2, N_TILES, 2):
            b, s = divmod(p - 2, 4)
            for g in range(2):
                later(post, p, quant_z, b, g, s, 2)
        for half in range(2):
            later(scalar_early, 0, copy_x, 1, half, "s")
        later(post, 0, quant_x, 1)
        x_steps = ((2, 3, "s"), ((3, 0), 5, "s"), ((3, 1), 7, "s"), (4, 11, "v"))
        for key, p, engine in x_steps:
            for half in range(2):
                later(end_work, p, turn_x, key, half, ("xt", "dec")[half])
                later(scalar_early, p + 1, copy_x, key, half, engine)
            later(post, p + 1, quant_x, key)
        for i in range(8):
            p = (1, 2, 3, 4, 5, 6, 7, 8)[i]
            later(pool_work, p, group_w, u_chunks[i], "p")
            later(post, p + 1, quant_w, u_chunks[i])
        later(end_work, 6, make_bias, 2, ("u", 0), "v")
        later(end_work, 8, make_bias, 3, ("u", 1), "v")
        for i in range(6, N_TILES):
            later(loads, i - 6, load_noise, i)
        for i, p in ((2, 0), (3, 0), (4, 1), (5, 2), (6, 3), (7, 4)):
            later(loads, p, load_u_chunk, i)
        later(loads, 2, load_x, (3, 1), xu, 0, 512)
        later(loads, 4, load_x, 4, xv, 1536, 0)

        dec_tiles = [(b, i) for b in (0, 1, 2, 4) for i in range(4)]
        early = dec_tiles[:6]
        for n, (b, i) in enumerate(early):
            p = 17 + n // 2
            later(mid_work, p, emit_dec, b, i, "xt" if n % 2 else "dec")
            later(post, p, dec_add, b, i)

        cuc = sbt([P, 4], F32, "cuc")

        def make_cuc():
            curf = sbt([P, P], F32, "curf")
            nc.vector.tensor_copy(out=curf[:], in_=cur[:])
            cb = bank("dec")
            nc.tensor.transpose(cb[:, 0:P], curf[:], ident[:])
            nc.vector.tensor_copy(out=cuc[:], in_=cb[:, 0:4])

        def first_means():
            for g in range(2):
                quant_w(("v", 1, 0, g))
                emit_mean(0, g)
            for g in range(2):
                mean_add(0, g)
            for g in range(2):
                emit_mean(1, g)

        later(pre, 0, first_means)
        later(post, 14, make_cuc)
        for p in range(N_TILES):
            act_lv(p)
            for g in range(2):
                if not en_on_vector(p, g):
                    noise_product(nc.gpsimd, p, g)
            run(pool_work, p)
            run(pre, p)
            run(scalar_early, p)
            if p >= 1:
                for g in range(2):
                    turn_z(p - 1, g)
            if 1 < p + 1 < N_TILES:
                for g in range(2):
                    lv_add(p + 1, g)
            if p + 2 < N_TILES:
                for g in range(2):
                    emit_lv(p + 2, g)
            if p + 1 < N_TILES:
                for g in range(2):
                    mean_add(p + 1, g)
            if p + 2 < N_TILES:
                for g in range(2):
                    emit_mean(p + 2, g)
            if p >= 1:
                act_sq(p - 1)
            run(mid_work, p)
            run(scalar_work, p)
            if p >= 1:
                for g in range(2):
                    z_out(p - 1, g)
            for g in range(2):
                if en_on_vector(p, g):
                    noise_product(nc.vector, p, g)
            run(post, p)
            run(end_work, p)
            run(loads, p)
            if p == 4:
                nc.sync.dma_start(out=cvb[:], in_=cv.partition_broadcast(P))

        last = N_TILES - 1
        rest = dec_tiles[6:]
        spare = []
        for n in range(3):
            em = sbt([P, 2, L], F32, "em", 4)
            spare.extend(em[:, a, 512 * g : 512 * g + 512] for a in range(2) for g in range(2))
        tags = ("dec", "xt", "lv", "lv", "mean", "mean", "dec", "xt", "lv", "lv")
        for g in range(2):
            turn_z(last, g)
            if g == 0:
                for n in range(2):
                    emit_dec(*rest[n], tags[n])
        for b, i in early:
            dec_store(b, i)
        for n in range(2, 6):
            emit_dec(*rest[n], tags[n])
        for n in range(2):
            dec_add(*rest[n], spare[n])
            z_out(last, n)
        for g in range(2):
            quant_z(4, g, 2, 2)
        for n in range(2):
            dec_store(*rest[n])
        act_sq(last)
        for n in range(2, 6):
            dec_add(*rest[n], spare[n])
            dec_store(*rest[n])
        for n in range(6, 10):
            emit_dec(*rest[n], tags[n])
        klc = sbt([P, P], F32, "klc")
        nc.gpsimd.memset(klc[:], 0.0)
        for n in range(6, 10):
            dec_add(*rest[n], spare[n])
            dec_store(*rest[n])
        kls = sbt([P, 2, N_TILES], F32, "kls")
        for n in range(2):
            nc.vector.tensor_tensor(kls[:, n, :], sums[n][:, 0, :], sums[n][:, 1, :], ALU.add)
        nc.vector.tensor_scalar(kls[:, 1, :], kls[:, 1, :], 0.5, None, ALU.mult)
        nc.vector.tensor_tensor(kls[:, 1, :], kls[:, 1, :], kls[:, 0, :], ALU.subtract)
        nc.vector.tensor_scalar(klc[:, 0:N_TILES], kls[:, 1, :], 1.0 / L, -0.5, ALU.mult, ALU.add)
        kb = bank("mean")
        nc.tensor.transpose(kb[:, 0:P], klc[:], ident[:])
        klt = sbt([P, P], F32, "klt")
        nc.vector.tensor_copy(out=klt[:], in_=kb[:, 0:P])
        nc.sync.dma_start(out=kl_u.rearrange("(j r) -> j r", r=P), in_=klt[0:4, :])
        nc.sync.dma_start(out=kl_v.rearrange("(j r) -> j r", r=P), in_=klt[4:20, :])
